import numpy as np
import ml_dtypes


def mxq(x, axis, fmt="e4m3"):
    dtype, down = {"e4m3": (ml_dtypes.float8_e4m3fn, 7), "e5m2": (ml_dtypes.float8_e5m2, 14)}[fmt]
    v = np.moveaxis(np.asarray(x, np.float32).astype(ml_dtypes.bfloat16).astype(np.float64), axis, -1)
    blocks = v.reshape(v.shape[:-1] + (-1, 32))
    amax = np.abs(blocks).max(-1, keepdims=True)
    byte = np.maximum(np.where(amax > 0, np.frexp(amax)[1] - 1 + 127, 0) - down, 1)
    scale = np.exp2(byte - 127.0)
    codes = (blocks / scale).astype(np.float32).astype(dtype).astype(np.float64)
    return np.moveaxis((codes * scale).reshape(v.shape), -1, axis)


WIDE = False


def mx_kscale(k):
    if not WIDE:
        return np.ones(k)
    levels = np.array([18, -18])
    if k % 512:
        return np.exp2(np.random.permutation(np.resize(levels, k // 32))).repeat(32)
    a = np.empty((k // 512, 16))
    for p in range(k // 512):
        a[p, :8] = np.random.permutation(np.resize(levels, 8))
        for g in range(8):
            far = levels[np.abs(levels - a[p, g]) >= 10]
            a[p, g + 8] = far[np.random.randint(len(far))]
    return np.exp2(a.ravel()).repeat(32)


def f64(x):
    return np.asarray(x).astype(np.float64)


def striped(idx):
    return np.tile(np.asarray(idx).reshape(-1, 16).T, (8, 1)).astype(np.uint16)


def unstriped(offs):
    return offs[:16].T.reshape(-1).astype(np.int64)


N, T, D, V = 512, 2048, 512, 512


def setup_inputs():
    n = np.random.standard_normal
    idx = np.random.permutation(T)[:N]
    s = mx_kscale(D)[:, None]
    z = mx_kscale(V)[:, None]
    w = n((D, V)) / np.sqrt(D)
    return {
        "xT": (n((D, T)) / s).astype(np.float32),
        "wd": (w * s).astype(np.float32),
        "wv": (w.T / z).astype(np.float32),
        "y": (2 * np.random.randint(0, 2, (V, N)) - 1).astype(np.float32),
        "cw": (np.random.uniform(0.5, 1.5, (V, 1)) / np.sqrt(V) * z).astype(np.float32),
        "rw": np.tile(np.random.uniform(0.5, 1.5, N), (128, 1)).astype(np.float32),
        "offs": striped(idx),
    }


def reference(xT, wd, wv, y, cw, rw, offs):
    idx = unstriped(offs)
    a = mxq(f64(wd), 0, "e4m3").T @ mxq(f64(xT)[:, idx], 0, "e4m3")
    g = -f64(cw) * f64(rw)[:1] * f64(y) * np.maximum(1.0 - f64(y) * a, 0.0)
    dx = mxq(f64(wv), 0, "e4m3").T @ mxq(g, 0, "e5m2")
    gx = np.zeros((D, T))
    gx[:, idx] = dx
    return gx

@@ -1,0 +1,189 @@
+from contextlib import ExitStack
+
+import concourse.mybir as mybir
+
+N, T, D, V = 512, 2048, 512, 512
+FLOPS = 2 * D * V * N + 2 * V * D * N
+
+F32 = mybir.dt.float32
+BF16 = mybir.dt.bfloat16
+U32 = mybir.dt.uint32
+U16 = mybir.dt.uint16
+U8 = mybir.dt.uint8
+E4 = mybir.dt.float8_e4m3fn_x4
+E5 = mybir.dt.float8_e5m2_x4
+MULT = mybir.AluOpType.mult
+RELU = mybir.ActivationFunctionType.Relu
+
+P = 128
+PACK = 4
+HALF = N // 2
+LIST_HALF = HALF // 16
+
+
+def tile_attend_gml_sqh_kernel(tc, xT, wd, wv, y, cw, rw, offs, out):
+    nc = tc.nc
+    with ExitStack() as ctx:
+        keep = ctx.enter_context(tc.tile_pool(name="keep", bufs=1))
+        psum = ctx.enter_context(tc.psum_pool(name="psum", bufs=1))
+
+        offsets = keep.tile([P, N // 16], U16, name="offsets")
+        x_planes = [keep.tile([P, T], F32, name=f"x_plane{t}") for t in range(PACK)]
+        wd_raw = keep.tile([P, PACK, V], F32, name="wd_raw")
+        wv_raw = keep.tile([P, PACK, D], F32, name="wv_raw")
+        y_pairs = [keep.tile([P, 2, N], F32, name=f"y_pair{u}") for u in range(2)]
+        cw_raw = keep.tile([P, PACK], F32, name="cw_raw")
+        rw_rows = keep.tile([P, N], F32, name="rw_rows")
+        windows = [keep.tile([P, T], F32, name=f"window{q}") for q in range(PACK)]
+
+        x_rows = xT.rearrange("(p t) w -> p t w", t=PACK)
+        y_rows = y.rearrange("(p t) n -> p t n", t=PACK)
+        nc.sync.dma_start(out=x_planes[0][:], in_=x_rows[:, 0, :])
+        nc.sync.dma_start(offsets[:], offs)
+        nc.sync.dma_start(out=cw_raw[:], in_=cw.rearrange("(p t) o -> p (t o)", t=PACK))
+        nc.sync.dma_start(out=wd_raw[:], in_=wd.rearrange("(p j) c -> p j c", j=PACK))
+        for t in range(1, PACK):
+            nc.sync.dma_start(out=x_planes[t][:], in_=x_rows[:, t, :])
+        nc.sync.dma_start(out=rw_rows[:], in_=rw)
+        for u in range(2):
+            nc.sync.dma_start(out=y_pairs[u][:], in_=y_rows[:, 2 * u : 2 * u + 2, :])
+        nc.sync.dma_start(out=wv_raw[:], in_=wv.rearrange("(p j) c -> p j c", j=PACK))
+
+        g_codes = keep.tile([P, HALF + N], U32, name="g_codes", align_bytes=64)
+        g_scales = keep.tile([P, HALF + N], U8, name="g_scales", align_bytes=64)
+        for q in range(PACK):
+            nc.vector.memset(windows[q][:].bitcast(U32), 0)
+        nc.vector.memset(g_codes[:, 0:HALF], 0)
+        nc.vector.memset(g_scales[:, 0:HALF].bitcast(U32), 0)
+
+        wd_grouped = keep.tile([P, PACK, P, PACK], BF16, name="wd_grouped", align_bytes=64)
+        nc.scalar.copy(
+            out=wd_grouped[:].rearrange("p t m j -> p m j t"),
+            in_=wd_raw[:].rearrange("p j (m t) -> p m j t", t=PACK),
+        )
+        x_grouped = keep.tile([P, N, PACK], BF16, name="x_grouped", align_bytes=64)
+        neg_cw = keep.tile([P, PACK], F32, name="neg_cw")
+        wd_codes = keep.tile([P, V], U32, name="wd_codes", align_bytes=64)
+        wd_scales = keep.tile([P, V], U8, name="wd_scales", align_bytes=64)
+        x_codes = keep.tile([P, N], U32, name="x_codes", align_bytes=64)
+        x_scales = keep.tile([P, N], U8, name="x_scales", align_bytes=64)
+
+        nc.vector.tensor_copy(out=x_grouped[:, :, 0], in_=x_planes[0][:].indirect(offsets[:]))
+        nc.vector.tensor_scalar(out=neg_cw[:], in0=cw_raw[:], scalar1=-1.0, scalar2=None, op0=MULT)
+        nc.vector.tensor_copy(out=x_grouped[:, :, 1], in_=x_planes[1][:].indirect(offsets[:]))
+        nc.vector.quantize_mx(
+            out=wd_codes[:].bitcast(E4),
+            scales=wd_scales[:],
+            in_=wd_grouped[:].rearrange("p t m j -> p (t m j)"),
+        )
+        for t in range(2, PACK):
+            nc.vector.tensor_copy(out=x_grouped[:, :, t], in_=x_planes[t][:].indirect(offsets[:]))
+        nc.vector.quantize_mx(
+            out=x_codes[:].bitcast(E4),
+            scales=x_scales[:],
+            in_=x_grouped[:].rearrange("p n t -> p (n t)"),
+        )
+
+        margin = keep.tile([P, PACK, N], F32, name="margin")
+        hinge = keep.tile([P, PACK, N], F32, name="hinge")
+        weight = keep.tile([P, PACK, N], F32, name="weight")
+        for t in range(PACK):
+            a_bank = psum.tile([P, N], F32, name=f"a_bank{t}")
+            cols = slice(t * P, (t + 1) * P)
+            nc.tensor.matmul_mx(
+                out=a_bank[:],
+                lhsT=wd_codes[:, cols].bitcast(E4),
+                lhsT_scale=wd_scales[:, cols],
+                rhs=x_codes[:].bitcast(E4),
+                rhs_scale=x_scales[:],
+                start=True,
+                stop=True,
+            )
+            nc.vector.tensor_tensor(out=margin[:, t, :], in0=a_bank[:], in1=y_pairs[t // 2][:, t % 2, :], op=MULT)
+            nc.scalar.activation(out=hinge[:, t, :], in_=margin[:, t, :], func=RELU, bias=1.0, scale=-1.0)
+        for t in range(PACK):
+            nc.vector.scalar_tensor_tensor(
+                out=weight[:, t, :],
+                in0=y_pairs[t // 2][:, t % 2, :],
+                scalar=neg_cw[:, t : t + 1],
+                in1=rw_rows[:],
+                op0=MULT,
+                op1=MULT,
+            )
+
+        wv_grouped = keep.tile([P, D, PACK], BF16, name="wv_grouped", align_bytes=64)
+        wv_codes = keep.tile([P, D], U32, name="wv_codes", align_bytes=64)
+        wv_scales = keep.tile([P, D], U8, name="wv_scales", align_bytes=64)
+        for q in range(PACK):
+            cols = slice(q * P, (q + 1) * P)
+            nc.scalar.copy(
+                out=wv_grouped[:, cols, :].rearrange("p (c i) j -> p c j i", i=4),
+                in_=wv_raw[:, :, cols].rearrange("p j (c i) -> p c j i", i=4),
+            )
+
+        def quantize_wv(q):
+            cols = slice(q * P, (q + 1) * P)
+            nc.vector.quantize_mx(
+                out=wv_codes[:, cols].bitcast(E4),
+                scales=wv_scales[:, cols],
+                in_=wv_grouped[:, cols, :].rearrange("p c j -> p (c j)"),
+            )
+
+        g_grouped = keep.tile([P, N, PACK], BF16, name="g_grouped", align_bytes=64)
+
+        def make_g(h):
+            cols = slice(h * HALF, (h + 1) * HALF)
+            nc.vector.tensor_tensor(
+                out=g_grouped[:, cols, :].rearrange("p (c i) t -> p c t i", i=4),
+                in0=hinge[:, :, cols].rearrange("p t (c i) -> p c t i", i=4),
+                in1=weight[:, :, cols].rearrange("p t (c i) -> p c t i", i=4),
+                op=MULT,
+            )
+
+        def quantize_g(h):
+            cols = slice(h * HALF, (h + 1) * HALF)
+            to = slice((h + 1) * HALF, (h + 2) * HALF)
+            nc.vector.quantize_mx(
+                out=g_codes[:, to].bitcast(E5),
+                scales=g_scales[:, to],
+                in_=g_grouped[:, cols, :].rearrange("p n t -> p (n t)"),
+            )
+
+        def second_product(bank, q, first):
+            cols = slice(q * P, (q + 1) * P)
+            nc.tensor.matmul_mx(
+                out=bank[:],
+                lhsT=wv_codes[:, cols].bitcast(E4),
+                lhsT_scale=wv_scales[:, cols],
+                rhs=g_codes[:, first : first + N].bitcast(E5),
+                rhs_scale=g_scales[:, first : first + N],
+                start=True,
+                stop=True,
+            )
+
+        make_g(0)
+        quantize_wv(0)
+        quantize_g(0)
+        make_g(1)
+        quantize_wv(1)
+        quantize_g(1)
+        quantize_wv(2)
+        quantize_wv(3)
+
+        dx = [keep.tile([P, N], F32, name=f"dx{q}") for q in range(PACK)]
+        early_bank = psum.tile([P, N], F32, name="early_bank")
+        second_product(early_bank, 0, 0)
+        nc.scalar.copy(out=dx[0][:, 0:HALF], in_=early_bank[:, HALF:N])
+        nc.vector.tensor_copy(out=windows[0][:].indirect(offsets[:, 0:LIST_HALF]), in_=dx[0][:, 0:HALF])
+        for q in range(PACK):
+            dx_bank = psum.tile([P, N], F32, name=f"a_bank{q}")
+            second_product(dx_bank, q, HALF)
+            if q == 0:
+                nc.scalar.copy(out=dx[0][:, HALF:N], in_=dx_bank[:, HALF:N])
+                nc.vector.tensor_copy(
+                    out=windows[0][:].indirect(offsets[:, LIST_HALF : 2 * LIST_HALF]), in_=dx[0][:, HALF:N]
+                )
+            else:
+                nc.scalar.copy(out=dx[q][:], in_=dx_bank[:])
+                nc.vector.tensor_copy(out=windows[q][:].indirect(offsets[:]), in_=dx[q][:])
+            nc.sync.dma_start(out=out[q * P : (q + 1) * P, :], in_=windows[q][:])

@@ -1,6 +1,7 @@
 from contextlib import ExitStack
 
 import concourse.mybir as mybir
+from concourse.masks import make_identity
 
 N, T, D, V = 512, 2048, 512, 512
 FLOPS = 2 * D * V * N + 2 * V * D * N
@@ -13,11 +14,13 @@ U8 = mybir.dt.uint8
 E4 = mybir.dt.float8_e4m3fn_x4
 E5 = mybir.dt.float8_e5m2_x4
 MULT = mybir.AluOpType.mult
+COPY = mybir.ActivationFunctionType.Copy
 RELU = mybir.ActivationFunctionType.Relu
 
 P = 128
 PACK = 4
 HALF = N // 2
+WD_VECTOR = 88
 LIST_HALF = HALF // 16
 
 
@@ -33,7 +36,7 @@ def tile_attend_gml_sqh_kernel(tc, xT, wd, wv, y, cw, rw, offs, out):
         wv_raw = keep.tile([P, PACK, D], F32, name="wv_raw")
         y_pairs = [keep.tile([P, 2, N], F32, name=f"y_pair{u}") for u in range(2)]
         cw_raw = keep.tile([P, PACK], F32, name="cw_raw")
-        rw_rows = keep.tile([P, N], F32, name="rw_rows")
+        rw_raw = keep.tile([P, PACK], F32, name="rw_raw")
         windows = [keep.tile([P, T], F32, name=f"window{q}") for q in range(PACK)]
 
         x_rows = xT.rearrange("(p t) w -> p t w", t=PACK)
@@ -41,47 +44,61 @@ def tile_attend_gml_sqh_kernel(tc, xT, wd, wv, y, cw, rw, offs, out):
         nc.sync.dma_start(out=x_planes[0][:], in_=x_rows[:, 0, :])
         nc.sync.dma_start(offsets[:], offs)
         nc.sync.dma_start(out=cw_raw[:], in_=cw.rearrange("(p t) o -> p (t o)", t=PACK))
-        nc.sync.dma_start(out=wd_raw[:], in_=wd.rearrange("(p j) c -> p j c", j=PACK))
+        nc.sync.dma_start(out=rw_raw[:], in_=rw[0:1, :].rearrange("o (p j) -> (o p) j", j=PACK))
         for t in range(1, PACK):
             nc.sync.dma_start(out=x_planes[t][:], in_=x_rows[:, t, :])
-        nc.sync.dma_start(out=rw_rows[:], in_=rw)
+        nc.sync.dma_start(out=wd_raw[:], in_=wd.rearrange("(p j) c -> p j c", j=PACK))
         for u in range(2):
             nc.sync.dma_start(out=y_pairs[u][:], in_=y_rows[:, 2 * u : 2 * u + 2, :])
         nc.sync.dma_start(out=wv_raw[:], in_=wv.rearrange("(p j) c -> p j c", j=PACK))
 
         g_codes = keep.tile([P, HALF + N], U32, name="g_codes", align_bytes=64)
         g_scales = keep.tile([P, HALF + N], U8, name="g_scales", align_bytes=64)
+        identity = keep.tile([P, P], F32, name="identity")
+        make_identity(nc, identity[:])
         for q in range(PACK):
-            nc.vector.memset(windows[q][:].bitcast(U32), 0)
+            engine = nc.vector if q < 2 else nc.gpsimd
+            engine.memset(windows[q][:].bitcast(U32), 0)
         nc.vector.memset(g_codes[:, 0:HALF], 0)
         nc.vector.memset(g_scales[:, 0:HALF].bitcast(U32), 0)
 
-        wd_grouped = keep.tile([P, PACK, P, PACK], BF16, name="wd_grouped", align_bytes=64)
-        nc.scalar.copy(
-            out=wd_grouped[:].rearrange("p t m j -> p m j t"),
-            in_=wd_raw[:].rearrange("p j (m t) -> p m j t", t=PACK),
-        )
-        x_grouped = keep.tile([P, N, PACK], BF16, name="x_grouped", align_bytes=64)
         neg_cw = keep.tile([P, PACK], F32, name="neg_cw")
+        nc.vector.tensor_scalar(out=neg_cw[:], in0=cw_raw[:], scalar1=-1.0, scalar2=None, op0=MULT)
+        rw_bank = psum.tile([P, PACK, P], F32, name="rw_bank")
+        for j in range(PACK):
+            nc.tensor.transpose(rw_bank[:, j, :], rw_raw[:, j : j + 1].to_broadcast([P, P]), identity[:])
+        outer = keep.tile([P, PACK, N], F32, name="outer")
+        for t in range(PACK):
+            nc.scalar.activation(
+                out=outer[:, t, :].rearrange("p (n j) -> p n j", j=PACK),
+                in_=rw_bank[:].rearrange("p j n -> p n j"),
+                func=COPY,
+                scale=neg_cw[:, t : t + 1],
+            )
+
+        wd_grouped = keep.tile([P, PACK, P, PACK], BF16, name="wd_grouped", align_bytes=64)
+        wd_to = wd_grouped[:].rearrange("p t m j -> p m j t")
+        wd_from = wd_raw[:].rearrange("p j (m t) -> p m j t", t=PACK)
+        x_grouped = keep.tile([P, N, PACK], BF16, name="x_grouped", align_bytes=64)
         wd_codes = keep.tile([P, V], U32, name="wd_codes", align_bytes=64)
         wd_scales = keep.tile([P, V], U8, name="wd_scales", align_bytes=64)
         x_codes = keep.tile([P, N], U32, name="x_codes", align_bytes=64)
         x_scales = keep.tile([P, N], U8, name="x_scales", align_bytes=64)
 
-        nc.vector.tensor_copy(out=x_grouped[:, :, 0], in_=x_planes[0][:].indirect(offsets[:]))
-        nc.vector.tensor_scalar(out=neg_cw[:], in0=cw_raw[:], scalar1=-1.0, scalar2=None, op0=MULT)
-        nc.vector.tensor_copy(out=x_grouped[:, :, 1], in_=x_planes[1][:].indirect(offsets[:]))
-        nc.vector.quantize_mx(
-            out=wd_codes[:].bitcast(E4),
-            scales=wd_scales[:],
-            in_=wd_grouped[:].rearrange("p t m j -> p (t m j)"),
-        )
-        for t in range(2, PACK):
+        for t in range(PACK):
             nc.vector.tensor_copy(out=x_grouped[:, :, t], in_=x_planes[t][:].indirect(offsets[:]))
         nc.vector.quantize_mx(
             out=x_codes[:].bitcast(E4),
             scales=x_scales[:],
             in_=x_grouped[:].rearrange("p n t -> p (n t)"),
+        )
+
+        nc.vector.tensor_copy(out=wd_to[:, 0:WD_VECTOR], in_=wd_from[:, 0:WD_VECTOR])
+        nc.scalar.copy(out=wd_to[:, WD_VECTOR:P], in_=wd_from[:, WD_VECTOR:P])
+        nc.vector.quantize_mx(
+            out=wd_codes[:].bitcast(E4),
+            scales=wd_scales[:],
+            in_=wd_grouped[:].rearrange("p t m j -> p (t m j)"),
         )
 
         margin = keep.tile([P, PACK, N], F32, name="margin")
@@ -101,15 +118,9 @@ def tile_attend_gml_sqh_kernel(tc, xT, wd, wv, y, cw, rw, offs, out):
             )
             nc.vector.tensor_tensor(out=margin[:, t, :], in0=a_bank[:], in1=y_pairs[t // 2][:, t % 2, :], op=MULT)
             nc.scalar.activation(out=hinge[:, t, :], in_=margin[:, t, :], func=RELU, bias=1.0, scale=-1.0)
-        for t in range(PACK):
-            nc.vector.scalar_tensor_tensor(
-                out=weight[:, t, :],
-                in0=y_pairs[t // 2][:, t % 2, :],
-                scalar=neg_cw[:, t : t + 1],
-                in1=rw_rows[:],
-                op0=MULT,
-                op1=MULT,
-            )
+        for u in range(2):
+            pair = slice(2 * u, 2 * u + 2)
+            nc.vector.tensor_tensor(out=weight[:, pair, :], in0=y_pairs[u][:], in1=outer[:, pair, :], op=MULT)
 
         wv_grouped = keep.tile([P, D, PACK], BF16, name="wv_grouped", align_bytes=64)
         wv_codes = keep.tile([P, D], U32, name="wv_codes", align_bytes=64)
@@ -121,8 +132,8 @@ def tile_attend_gml_sqh_kernel(tc, xT, wd, wv, y, cw, rw, offs, out):
                 in_=wv_raw[:, :, cols].rearrange("p j (c i) -> p c j i", i=4),
             )
 
-        def quantize_wv(q):
-            cols = slice(q * P, (q + 1) * P)
+        def quantize_wv(u):
+            cols = slice(2 * u * P, 2 * (u + 1) * P)
             nc.vector.quantize_mx(
                 out=wv_codes[:, cols].bitcast(E4),
                 scales=wv_scales[:, cols],
@@ -167,8 +178,6 @@ def tile_attend_gml_sqh_kernel(tc, xT, wd, wv, y, cw, rw, offs, out):
         make_g(1)
         quantize_wv(1)
         quantize_g(1)
-        quantize_wv(2)
-        quantize_wv(3)
 
         dx = [keep.tile([P, N], F32, name=f"dx{q}") for q in range(PACK)]
         early_bank = psum.tile([P, N], F32, name="early_bank")

@@ -21,7 +21,6 @@ P = 128
 PACK = 4
 HALF = N // 2
 WD_VECTOR = 88
-LIST_HALF = HALF // 16
 
 
 def tile_attend_gml_sqh_kernel(tc, xT, wd, wv, y, cw, rw, offs, out):
@@ -43,8 +42,8 @@ def tile_attend_gml_sqh_kernel(tc, xT, wd, wv, y, cw, rw, offs, out):
         y_rows = y.rearrange("(p t) n -> p t n", t=PACK)
         nc.sync.dma_start(out=x_planes[0][:], in_=x_rows[:, 0, :])
         nc.sync.dma_start(offsets[:], offs)
-        nc.sync.dma_start(out=cw_raw[:], in_=cw.rearrange("(p t) o -> p (t o)", t=PACK))
-        nc.sync.dma_start(out=rw_raw[:], in_=rw[0:1, :].rearrange("o (p j) -> (o p) j", j=PACK))
+        nc.scalar.dma_start(out=cw_raw[:], in_=cw.rearrange("(p t) o -> p (t o)", t=PACK))
+        nc.scalar.dma_start(out=rw_raw[:], in_=rw[0:1, :].rearrange("o (p j) -> (o p) j", j=PACK))
         for t in range(1, PACK):
             nc.sync.dma_start(out=x_planes[t][:], in_=x_rows[:, t, :])
         nc.sync.dma_start(out=wd_raw[:], in_=wd.rearrange("(p j) c -> p j c", j=PACK))
@@ -67,7 +66,9 @@ def tile_attend_gml_sqh_kernel(tc, xT, wd, wv, y, cw, rw, offs, out):
         rw_bank = psum.tile([P, PACK, P], F32, name="rw_bank")
         for j in range(PACK):
             nc.tensor.transpose(rw_bank[:, j, :], rw_raw[:, j : j + 1].to_broadcast([P, P]), identity[:])
-        outer = keep.tile([P, PACK, N], F32, name="outer")
+        factors = keep.tile([P, PACK + 2, N], F32, name="factors")
+        outer = factors[:, 2 : PACK + 2, :]
+        weight = factors[:, 0:PACK, :]
         for t in range(PACK):
             nc.scalar.activation(
                 out=outer[:, t, :].rearrange("p (n j) -> p n j", j=PACK),
@@ -101,39 +102,49 @@ def tile_attend_gml_sqh_kernel(tc, xT, wd, wv, y, cw, rw, offs, out):
             in_=wd_grouped[:].rearrange("p t m j -> p (t m j)"),
         )
 
-        margin = keep.tile([P, PACK, N], F32, name="margin")
-        hinge = keep.tile([P, PACK, N], F32, name="hinge")
-        weight = keep.tile([P, PACK, N], F32, name="weight")
-        for t in range(PACK):
-            a_bank = psum.tile([P, N], F32, name=f"a_bank{t}")
-            cols = slice(t * P, (t + 1) * P)
-            nc.tensor.matmul_mx(
-                out=a_bank[:],
-                lhsT=wd_codes[:, cols].bitcast(E4),
-                lhsT_scale=wd_scales[:, cols],
-                rhs=x_codes[:].bitcast(E4),
-                rhs_scale=x_scales[:],
-                start=True,
-                stop=True,
-            )
-            nc.vector.tensor_tensor(out=margin[:, t, :], in0=a_bank[:], in1=y_pairs[t // 2][:, t % 2, :], op=MULT)
-            nc.scalar.activation(out=hinge[:, t, :], in_=margin[:, t, :], func=RELU, bias=1.0, scale=-1.0)
-        for u in range(2):
-            pair = slice(2 * u, 2 * u + 2)
-            nc.vector.tensor_tensor(out=weight[:, pair, :], in0=y_pairs[u][:], in1=outer[:, pair, :], op=MULT)
-
         wv_grouped = keep.tile([P, D, PACK], BF16, name="wv_grouped", align_bytes=64)
         wv_codes = keep.tile([P, D], U32, name="wv_codes", align_bytes=64)
         wv_scales = keep.tile([P, D], U8, name="wv_scales", align_bytes=64)
-        for q in range(PACK):
+
+        def round_wv(q):
             cols = slice(q * P, (q + 1) * P)
             nc.scalar.copy(
                 out=wv_grouped[:, cols, :].rearrange("p (c i) j -> p c j i", i=4),
                 in_=wv_raw[:, :, cols].rearrange("p j (c i) -> p c j i", i=4),
             )
 
-        def quantize_wv(u):
-            cols = slice(2 * u * P, 2 * (u + 1) * P)
+        margin = keep.tile([P, PACK, N], F32, name="margin")
+        hinge = keep.tile([P, PACK, N], F32, name="hinge")
+        nc.vector.tensor_tensor(out=weight[:, 0:2, :], in0=y_pairs[0][:], in1=outer[:, 0:2, :], op=MULT)
+        for h in range(2):
+            half = slice(h * HALF, (h + 1) * HALF)
+            nc.gpsimd.tensor_tensor(out=weight[:, 2:4, half], in0=y_pairs[1][:, :, half], in1=outer[:, 2:4, half], op=MULT)
+        for h in range(2):
+            half = slice(h * HALF, (h + 1) * HALF)
+            if h == 1:
+                round_wv(0)
+                round_wv(1)
+            for u in range(2):
+                pair = slice(2 * u, 2 * u + 2)
+                a_bank = psum.tile([P, 2, HALF], F32, name=f"a_bank{2 * h + u}")
+                for e in range(2):
+                    cols = slice((2 * u + e) * P, (2 * u + e + 1) * P)
+                    nc.tensor.matmul_mx(
+                        out=a_bank[:, e, :],
+                        lhsT=wd_codes[:, cols].bitcast(E4),
+                        lhsT_scale=wd_scales[:, cols],
+                        rhs=x_codes[:, half].bitcast(E4),
+                        rhs_scale=x_scales[:, half],
+                        start=True,
+                        stop=True,
+                    )
+                nc.vector.tensor_tensor(out=margin[:, pair, half], in0=a_bank[:], in1=y_pairs[u][:, :, half], op=MULT)
+                nc.scalar.activation(
+                    out=hinge[:, pair, half], in_=margin[:, pair, half], func=RELU, bias=1.0, scale=-1.0
+                )
+
+        def quantize_wv(first, count):
+            cols = slice(first * P, (first + count) * P)
             nc.vector.quantize_mx(
                 out=wv_codes[:, cols].bitcast(E4),
                 scales=wv_scales[:, cols],
@@ -172,27 +183,36 @@ def tile_attend_gml_sqh_kernel(tc, xT, wd, wv, y, cw, rw, offs, out):
                 stop=True,
             )
 
-        make_g(0)
-        quantize_wv(0)
-        quantize_g(0)
-        make_g(1)
-        quantize_wv(1)
-        quantize_g(1)
-
         dx = [keep.tile([P, N], F32, name=f"dx{q}") for q in range(PACK)]
+
+        def late_product(q, cols):
+            dx_bank = psum.tile([P, N], F32, name=f"a_bank{q}")
+            second_product(dx_bank, q, HALF)
+            nc.scalar.copy(out=dx[q][:, cols], in_=dx_bank[:, cols])
+
+        def scatter(q, first, last):
+            nc.vector.tensor_copy(
+                out=windows[q][:].indirect(offsets[:, first // 16 : last // 16]), in_=dx[q][:, first:last]
+            )
+
+        make_g(0)
+        quantize_wv(0, 2)
+        quantize_g(0)
         early_bank = psum.tile([P, N], F32, name="early_bank")
         second_product(early_bank, 0, 0)
         nc.scalar.copy(out=dx[0][:, 0:HALF], in_=early_bank[:, HALF:N])
-        nc.vector.tensor_copy(out=windows[0][:].indirect(offsets[:, 0:LIST_HALF]), in_=dx[0][:, 0:HALF])
-        for q in range(PACK):
-            dx_bank = psum.tile([P, N], F32, name=f"a_bank{q}")
-            second_product(dx_bank, q, HALF)
-            if q == 0:
-                nc.scalar.copy(out=dx[0][:, HALF:N], in_=dx_bank[:, HALF:N])
-                nc.vector.tensor_copy(
-                    out=windows[0][:].indirect(offsets[:, LIST_HALF : 2 * LIST_HALF]), in_=dx[0][:, HALF:N]
-                )
-            else:
-                nc.scalar.copy(out=dx[q][:], in_=dx_bank[:])
-                nc.vector.tensor_copy(out=windows[q][:].indirect(offsets[:]), in_=dx[q][:])
+        round_wv(2)
+        round_wv(3)
+        make_g(1)
+        quantize_wv(2, 2)
+        quantize_g(1)
+        scatter(0, 0, HALF)
+        late_product(0, slice(HALF, N))
+        late_product(1, slice(0, N))
+        late_product(2, slice(0, N))
+        late_product(3, slice(0, N))
+        scatter(0, HALF, N)
+        nc.sync.dma_start(out=out[0:P, :], in_=windows[0][:])
+        for q in range(1, PACK):
+            scatter(q, 0, N)
             nc.sync.dma_start(out=out[q * P : (q + 1) * P, :], in_=windows[q][:])

@@ -20,7 +20,7 @@ RELU = mybir.ActivationFunctionType.Relu
 P = 128
 PACK = 4
 HALF = N // 2
-WD_VECTOR = 88
+WD_VECTOR = 84
 
 
 def tile_attend_gml_sqh_kernel(tc, xT, wd, wv, y, cw, rw, offs, out):
@@ -198,21 +198,24 @@ def tile_attend_gml_sqh_kernel(tc, xT, wd, wv, y, cw, rw, offs, out):
         make_g(0)
         quantize_wv(0, 2)
         quantize_g(0)
-        early_bank = psum.tile([P, N], F32, name="early_bank")
-        second_product(early_bank, 0, 0)
-        nc.scalar.copy(out=dx[0][:, 0:HALF], in_=early_bank[:, HALF:N])
+        for q in range(2):
+            early_bank = psum.tile([P, N], F32, name=f"early_bank{q}")
+            second_product(early_bank, q, 0)
+            nc.scalar.copy(out=dx[q][:, 0:HALF], in_=early_bank[:, HALF:N])
         round_wv(2)
         round_wv(3)
         make_g(1)
         quantize_wv(2, 2)
         quantize_g(1)
-        scatter(0, 0, HALF)
-        late_product(0, slice(HALF, N))
-        late_product(1, slice(0, N))
-        late_product(2, slice(0, N))
-        late_product(3, slice(0, N))
-        scatter(0, HALF, N)
-        nc.sync.dma_start(out=out[0:P, :], in_=windows[0][:])
-        for q in range(1, PACK):
-            scatter(q, 0, N)
-            nc.sync.dma_start(out=out[q * P : (q + 1) * P, :], in_=windows[q][:])
+        for q in range(2):
+            scatter(q, 0, HALF)
+        for q in range(PACK):
+            first = HALF if q < 2 else 0
+            late_product(q, slice(first, N))
+            scatter(q, first, N)
+            rows = slice(q * P, (q + 1) * P)
+            if q < PACK - 1:
+                nc.sync.dma_start(out=out[rows, :], in_=windows[q][:])
+            else:
+                nc.sync.dma_start(out=out[rows, 0 : T // 2], in_=windows[q][:, 0 : T // 2])
+                nc.scalar.dma_start(out=out[rows, T // 2 : T], in_=windows[q][:, T // 2 : T])

@@ -20,7 +20,8 @@ RELU = mybir.ActivationFunctionType.Relu
 P = 128
 PACK = 4
 HALF = N // 2
-WD_VECTOR = 84
+QUARTER = N // 4
+WD_EXTRA = 24
 
 
 def tile_attend_gml_sqh_kernel(tc, xT, wd, wv, y, cw, rw, offs, out):
@@ -32,14 +33,17 @@ def tile_attend_gml_sqh_kernel(tc, xT, wd, wv, y, cw, rw, offs, out):
         offsets = keep.tile([P, N // 16], U16, name="offsets")
         x_planes = [keep.tile([P, T], F32, name=f"x_plane{t}") for t in range(PACK)]
         wd_raw = keep.tile([P, PACK, V], F32, name="wd_raw")
-        wv_raw = keep.tile([P, PACK, D], F32, name="wv_raw")
-        y_pairs = [keep.tile([P, 2, N], F32, name=f"y_pair{u}") for u in range(2)]
+        wv_raw = [
+            keep.tile([P, PACK, D // 2], F32, name=f"wv_raw{u}", tag=f"late_stage{u}", align_bytes=64) for u in range(2)
+        ]
+        y_planes = keep.tile([P, PACK, N], F32, name="y_planes")
         cw_raw = keep.tile([P, PACK], F32, name="cw_raw")
         rw_raw = keep.tile([P, PACK], F32, name="rw_raw")
         windows = [keep.tile([P, T], F32, name=f"window{q}") for q in range(PACK)]
 
         x_rows = xT.rearrange("(p t) w -> p t w", t=PACK)
         y_rows = y.rearrange("(p t) n -> p t n", t=PACK)
+        wv_rows = wv.rearrange("(p j) c -> p j c", j=PACK)
         nc.sync.dma_start(out=x_planes[0][:], in_=x_rows[:, 0, :])
         nc.sync.dma_start(offsets[:], offs)
         nc.scalar.dma_start(out=cw_raw[:], in_=cw.rearrange("(p t) o -> p (t o)", t=PACK))
@@ -48,8 +52,9 @@ def tile_attend_gml_sqh_kernel(tc, xT, wd, wv, y, cw, rw, offs, out):
             nc.sync.dma_start(out=x_planes[t][:], in_=x_rows[:, t, :])
         nc.sync.dma_start(out=wd_raw[:], in_=wd.rearrange("(p j) c -> p j c", j=PACK))
         for u in range(2):
-            nc.sync.dma_start(out=y_pairs[u][:], in_=y_rows[:, 2 * u : 2 * u + 2, :])
-        nc.sync.dma_start(out=wv_raw[:], in_=wv.rearrange("(p j) c -> p j c", j=PACK))
+            nc.sync.dma_start(out=y_planes[:, 2 * u : 2 * u + 2, :], in_=y_rows[:, 2 * u : 2 * u + 2, :])
+        for u in range(2):
+            nc.sync.dma_start(out=wv_raw[u][:], in_=wv_rows[:, :, u * (D // 2) : (u + 1) * (D // 2)])
 
         g_codes = keep.tile([P, HALF + N], U32, name="g_codes", align_bytes=64)
         g_scales = keep.tile([P, HALF + N], U8, name="g_scales", align_bytes=64)
@@ -66,18 +71,25 @@ def tile_attend_gml_sqh_kernel(tc, xT, wd, wv, y, cw, rw, offs, out):
         rw_bank = psum.tile([P, PACK, P], F32, name="rw_bank")
         for j in range(PACK):
             nc.tensor.transpose(rw_bank[:, j, :], rw_raw[:, j : j + 1].to_broadcast([P, P]), identity[:])
-        factors = keep.tile([P, PACK + 2, N], F32, name="factors")
-        outer = factors[:, 2 : PACK + 2, :]
-        weight = factors[:, 0:PACK, :]
+        rw_all = rw_bank[:].rearrange("p j n -> p n j")
+        outer = keep.tile([P, PACK, HALF], F32, name="outer")
         for t in range(PACK):
             nc.scalar.activation(
                 out=outer[:, t, :].rearrange("p (n j) -> p n j", j=PACK),
-                in_=rw_bank[:].rearrange("p j n -> p n j"),
+                in_=rw_all[:, 0 : HALF // PACK, :],
                 func=COPY,
                 scale=neg_cw[:, t : t + 1],
             )
 
-        wd_grouped = keep.tile([P, PACK, P, PACK], BF16, name="wd_grouped", align_bytes=64)
+        outer_last = keep.tile([P, HALF], F32, name="outer_last")
+        nc.scalar.activation(
+            out=outer_last[:].rearrange("p (n j) -> p n j", j=PACK),
+            in_=rw_all[:, HALF // PACK : N // PACK, :],
+            func=COPY,
+            scale=neg_cw[:, PACK - 1 : PACK],
+        )
+
+        wd_grouped = keep.tile([P, PACK, P, PACK], BF16, name="wd_grouped", tag="wd_stage", align_bytes=64)
         wd_to = wd_grouped[:].rearrange("p t m j -> p m j t")
         wd_from = wd_raw[:].rearrange("p j (m t) -> p m j t", t=PACK)
         x_grouped = keep.tile([P, N, PACK], BF16, name="x_grouped", align_bytes=64)
@@ -86,133 +98,168 @@ def tile_attend_gml_sqh_kernel(tc, xT, wd, wv, y, cw, rw, offs, out):
         x_codes = keep.tile([P, N], U32, name="x_codes", align_bytes=64)
         x_scales = keep.tile([P, N], U8, name="x_scales", align_bytes=64)
 
-        for t in range(PACK):
+        for t in range(PACK - 1):
             nc.vector.tensor_copy(out=x_grouped[:, :, t], in_=x_planes[t][:].indirect(offsets[:]))
-        nc.vector.quantize_mx(
-            out=x_codes[:].bitcast(E4),
-            scales=x_scales[:],
-            in_=x_grouped[:].rearrange("p n t -> p (n t)"),
-        )
-
-        nc.vector.tensor_copy(out=wd_to[:, 0:WD_VECTOR], in_=wd_from[:, 0:WD_VECTOR])
-        nc.scalar.copy(out=wd_to[:, WD_VECTOR:P], in_=wd_from[:, WD_VECTOR:P])
-        nc.vector.quantize_mx(
-            out=wd_codes[:].bitcast(E4),
-            scales=wd_scales[:],
-            in_=wd_grouped[:].rearrange("p t m j -> p (t m j)"),
-        )
-
-        wv_grouped = keep.tile([P, D, PACK], BF16, name="wv_grouped", align_bytes=64)
-        wv_codes = keep.tile([P, D], U32, name="wv_codes", align_bytes=64)
-        wv_scales = keep.tile([P, D], U8, name="wv_scales", align_bytes=64)
-
-        def round_wv(q):
-            cols = slice(q * P, (q + 1) * P)
-            nc.scalar.copy(
-                out=wv_grouped[:, cols, :].rearrange("p (c i) j -> p c j i", i=4),
-                in_=wv_raw[:, :, cols].rearrange("p j (c i) -> p c j i", i=4),
+        for h in range(2):
+            nc.vector.tensor_copy(
+                out=x_grouped[:, h * HALF : (h + 1) * HALF, PACK - 1],
+                in_=x_planes[PACK - 1][:].indirect(offsets[:, h * HALF // 16 : (h + 1) * HALF // 16]),
             )
-
-        margin = keep.tile([P, PACK, N], F32, name="margin")
-        hinge = keep.tile([P, PACK, N], F32, name="hinge")
-        nc.vector.tensor_tensor(out=weight[:, 0:2, :], in0=y_pairs[0][:], in1=outer[:, 0:2, :], op=MULT)
         for h in range(2):
             half = slice(h * HALF, (h + 1) * HALF)
-            nc.gpsimd.tensor_tensor(out=weight[:, 2:4, half], in0=y_pairs[1][:, :, half], in1=outer[:, 2:4, half], op=MULT)
-        for h in range(2):
-            half = slice(h * HALF, (h + 1) * HALF)
-            if h == 1:
-                round_wv(0)
-                round_wv(1)
-            for u in range(2):
-                pair = slice(2 * u, 2 * u + 2)
-                a_bank = psum.tile([P, 2, HALF], F32, name=f"a_bank{2 * h + u}")
-                for e in range(2):
-                    cols = slice((2 * u + e) * P, (2 * u + e + 1) * P)
-                    nc.tensor.matmul_mx(
-                        out=a_bank[:, e, :],
-                        lhsT=wd_codes[:, cols].bitcast(E4),
-                        lhsT_scale=wd_scales[:, cols],
-                        rhs=x_codes[:, half].bitcast(E4),
-                        rhs_scale=x_scales[:, half],
-                        start=True,
-                        stop=True,
-                    )
-                nc.vector.tensor_tensor(out=margin[:, pair, half], in0=a_bank[:], in1=y_pairs[u][:, :, half], op=MULT)
-                nc.scalar.activation(
-                    out=hinge[:, pair, half], in_=margin[:, pair, half], func=RELU, bias=1.0, scale=-1.0
-                )
-
-        def quantize_wv(first, count):
-            cols = slice(first * P, (first + count) * P)
             nc.vector.quantize_mx(
-                out=wv_codes[:, cols].bitcast(E4),
-                scales=wv_scales[:, cols],
-                in_=wv_grouped[:, cols, :].rearrange("p c j -> p (c j)"),
+                out=x_codes[:, half].bitcast(E4),
+                scales=x_scales[:, half],
+                in_=x_grouped[:, half, :].rearrange("p n t -> p (n t)"),
             )
 
-        g_grouped = keep.tile([P, N, PACK], BF16, name="g_grouped", align_bytes=64)
-
-        def make_g(h):
-            cols = slice(h * HALF, (h + 1) * HALF)
-            nc.vector.tensor_tensor(
-                out=g_grouped[:, cols, :].rearrange("p (c i) t -> p c t i", i=4),
-                in0=hinge[:, :, cols].rearrange("p t (c i) -> p c t i", i=4),
-                in1=weight[:, :, cols].rearrange("p t (c i) -> p c t i", i=4),
-                op=MULT,
+        nc.vector.tensor_copy(out=wd_to[:, :, :, 0:2], in_=wd_from[:, :, :, 0:2])
+        nc.vector.tensor_copy(out=wd_to[:, 0:WD_EXTRA, :, 2:4], in_=wd_from[:, 0:WD_EXTRA, :, 2:4])
+        nc.scalar.copy(out=wd_to[:, WD_EXTRA:P, :, 2:4], in_=wd_from[:, WD_EXTRA:P, :, 2:4])
+        for u in range(2):
+            cols = slice(2 * u * P, (2 * u + 2) * P)
+            nc.vector.quantize_mx(
+                out=wd_codes[:, cols].bitcast(E4),
+                scales=wd_scales[:, cols],
+                in_=wd_grouped[:, 2 * u : 2 * u + 2].rearrange("p t m j -> p (t m j)"),
             )
 
-        def quantize_g(h):
-            cols = slice(h * HALF, (h + 1) * HALF)
+        def first_product(bank, t, cols):
+            nc.tensor.matmul_mx(
+                out=bank,
+                lhsT=wd_codes[:, t * P : (t + 1) * P].bitcast(E4),
+                lhsT_scale=wd_scales[:, t * P : (t + 1) * P],
+                rhs=x_codes[:, cols].bitcast(E4),
+                rhs_scale=x_scales[:, cols],
+                start=True,
+                stop=True,
+            )
+
+        def relu(hinge, margin):
+            nc.scalar.activation(out=hinge, in_=margin, func=RELU, bias=1.0, scale=-1.0)
+
+        def by_plane(planes):
+            return planes.rearrange("p t (c i) -> p c t i", i=4)
+
+        def by_word(words):
+            return words.rearrange("p (c i) t -> p c t i", i=4)
+
+        def quantize_wv(u, codes, scales):
+            nc.vector.quantize_mx(
+                out=codes[:].bitcast(E4), scales=scales[:], in_=wv_grouped[u][:].rearrange("p c j -> p (c j)")
+            )
+
+        def quantize_g(h, grouped):
             to = slice((h + 1) * HALF, (h + 2) * HALF)
             nc.vector.quantize_mx(
-                out=g_codes[:, to].bitcast(E5),
-                scales=g_scales[:, to],
-                in_=g_grouped[:, cols, :].rearrange("p n t -> p (n t)"),
+                out=g_codes[:, to].bitcast(E5), scales=g_scales[:, to], in_=grouped[:].rearrange("p n t -> p (n t)")
             )
 
-        def second_product(bank, q, first):
-            cols = slice(q * P, (q + 1) * P)
+        def second_product(bank, codes, scales, q, first):
+            cols = slice(q % 2 * P, (q % 2 + 1) * P)
             nc.tensor.matmul_mx(
                 out=bank[:],
-                lhsT=wv_codes[:, cols].bitcast(E4),
-                lhsT_scale=wv_scales[:, cols],
+                lhsT=codes[:, cols].bitcast(E4),
+                lhsT_scale=scales[:, cols],
                 rhs=g_codes[:, first : first + N].bitcast(E5),
                 rhs_scale=g_scales[:, first : first + N],
                 start=True,
                 stop=True,
             )
 
-        dx = [keep.tile([P, N], F32, name=f"dx{q}") for q in range(PACK)]
+        def scatter(q, values, first, last):
+            nc.vector.tensor_copy(out=windows[q][:].indirect(offsets[:, first // 16 : last // 16]), in_=values[:])
 
-        def late_product(q, cols):
-            dx_bank = psum.tile([P, N], F32, name=f"a_bank{q}")
-            second_product(dx_bank, q, HALF)
-            nc.scalar.copy(out=dx[q][:, cols], in_=dx_bank[:, cols])
+        weight = keep.tile([P, PACK, N], F32, name="weight", tag="wd_stage", align_bytes=64)
+        margins = [
+            keep.tile([P, PACK, HALF], F32, name=f"margin{h}", tag=f"wv_stage{h}", align_bytes=64) for h in range(2)
+        ]
+        hinge_h0 = keep.tile([P, PACK, HALF], F32, name="hinge_h0", tag="hinge_stage", align_bytes=64)
 
-        def scatter(q, first, last):
-            nc.vector.tensor_copy(
-                out=windows[q][:].indirect(offsets[:, first // 16 : last // 16]), in_=dx[q][:, first:last]
+        def vector_weight(t):
+            nc.vector.scalar_tensor_tensor(
+                out=weight[:, t, HALF:N].rearrange("p (n j) -> p n j", j=PACK),
+                in0=y_planes[:, t, HALF:N].rearrange("p (n j) -> p n j", j=PACK),
+                scalar=neg_cw[:, t : t + 1],
+                in1=rw_all[:, HALF // PACK : N // PACK, :],
+                op0=MULT,
+                op1=MULT,
             )
 
-        make_g(0)
-        quantize_wv(0, 2)
-        quantize_g(0)
-        for q in range(2):
-            early_bank = psum.tile([P, N], F32, name=f"early_bank{q}")
-            second_product(early_bank, q, 0)
-            nc.scalar.copy(out=dx[q][:, 0:HALF], in_=early_bank[:, HALF:N])
+        for u in range(2):
+            pair = slice(2 * u, 2 * u + 2)
+            nc.gpsimd.tensor_tensor(
+                out=weight[:, pair, 0:HALF], in0=y_planes[:, pair, 0:HALF], in1=outer[:, pair, :], op=MULT
+            )
+        nc.gpsimd.tensor_tensor(out=weight[:, 3, HALF:N], in0=y_planes[:, 3, HALF:N], in1=outer_last[:], op=MULT)
+        vector_weight(0)
+        vector_weight(1)
+        for h in range(2):
+            half = slice(h * HALF, (h + 1) * HALF)
+            for u in range(2):
+                pair = slice(2 * u, 2 * u + 2)
+                a_bank = psum.tile([P, 2, HALF], F32, name=f"a_bank{2 * h + u}")
+                for e in range(2):
+                    first_product(a_bank[:, e, :], 2 * u + e, half)
+                if h == 1 and u == 1:
+                    vector_weight(2)
+                nc.vector.tensor_tensor(out=margins[h][:, pair, :], in0=a_bank[:], in1=y_planes[:, pair, half], op=MULT)
+                if h == 0:
+                    relu(hinge_h0[:, pair, :], margins[h][:, pair, :])
+
+        wv_grouped = []
+
+        def round_wv(q):
+            if q % 2 == 0:
+                wv_grouped.append(
+                    keep.tile([P, D // 2, PACK], BF16, name=f"wv_grouped{q // 2}", tag=f"wv_stage{q // 2}", align_bytes=64)
+                )
+            cols = slice(q % 2 * P, (q % 2 + 1) * P)
+            nc.scalar.copy(out=by_word(wv_grouped[q // 2][:, cols, :]), in_=by_plane(wv_raw[q // 2][:, :, cols]))
+
+        round_wv(0)
+        round_wv(1)
+        hinge_h1 = keep.tile([P, PACK, HALF], F32, name="hinge_h1", tag="late_stage0", align_bytes=64)
+        for u in range(2):
+            relu(hinge_h1[:, 2 * u : 2 * u + 2, :], margins[1][:, 2 * u : 2 * u + 2, :])
         round_wv(2)
         round_wv(3)
-        make_g(1)
-        quantize_wv(2, 2)
-        quantize_g(1)
+
+        g_halves = [keep.tile([P, HALF, PACK], BF16, name=f"g_half{h}", align_bytes=64) for h in range(2)]
+
+        def make_g(h, hinge):
+            nc.vector.tensor_tensor(
+                out=by_word(g_halves[h][:]),
+                in0=by_plane(hinge[:]),
+                in1=by_plane(weight[:, :, h * HALF : (h + 1) * HALF]),
+                op=MULT,
+            )
+
+        make_g(0, hinge_h0)
+        wv_codes0 = keep.tile([P, D // 2], U32, name="wv_codes0", tag="hinge_stage", align_bytes=64)
+        wv_scales = [keep.tile([P, D // 2], U8, name=f"wv_scales{u}", align_bytes=64) for u in range(2)]
+        quantize_wv(0, wv_codes0, wv_scales[0])
+        quantize_g(0, g_halves[0])
+        early = []
         for q in range(2):
-            scatter(q, 0, HALF)
+            early_bank = psum.tile([P, N], F32, name=f"early_bank{q}")
+            second_product(early_bank, wv_codes0, wv_scales[0], q, 0)
+            early.append(keep.tile([P, HALF], F32, name=f"early{q}"))
+            nc.scalar.copy(out=early[q][:], in_=early_bank[:, HALF:N])
+        make_g(1, hinge_h1)
+        wv_codes1 = keep.tile([P, D // 2], U32, name="wv_codes1", tag="late_stage0", align_bytes=64)
+        quantize_wv(1, wv_codes1, wv_scales[1])
+        quantize_g(1, g_halves[1])
+        for q in range(2):
+            scatter(q, early[q], 0, HALF)
+        wv_codes = [wv_codes0, wv_codes1]
         for q in range(PACK):
             first = HALF if q < 2 else 0
-            late_product(q, slice(first, N))
-            scatter(q, first, N)
+            dx_bank = psum.tile([P, N], F32, name=f"a_bank{q}")
+            second_product(dx_bank, wv_codes[q // 2], wv_scales[q // 2], q, HALF)
+            dx = keep.tile([P, N - first], F32, name=f"dx{q}")
+            nc.scalar.copy(out=dx[:], in_=dx_bank[:, first:N])
+            scatter(q, dx, first, N)
             rows = slice(q * P, (q + 1) * P)
             if q < PACK - 1:
                 nc.sync.dma_start(out=out[rows, :], in_=windows[q][:])

@@ -34,7 +34,7 @@ def tile_attend_gml_sqh_kernel(tc, xT, wd, wv, y, cw, rw, offs, out):
         x_planes = [keep.tile([P, T], F32, name=f"x_plane{t}") for t in range(PACK)]
         wd_raw = keep.tile([P, PACK, V], F32, name="wd_raw")
         wv_raw = [
-            keep.tile([P, PACK, D // 2], F32, name=f"wv_raw{u}", tag=f"late_stage{u}", align_bytes=64) for u in range(2)
+            keep.tile([P, PACK, D // 2], F32, name=f"wv_raw{u}") for u in range(2)
         ]
         y_planes = keep.tile([P, PACK, N], F32, name="y_planes")
         cw_raw = keep.tile([P, PACK], F32, name="cw_raw")
@@ -172,9 +172,21 @@ def tile_attend_gml_sqh_kernel(tc, xT, wd, wv, y, cw, rw, offs, out):
 
         weight = keep.tile([P, PACK, N], F32, name="weight", tag="wd_stage", align_bytes=64)
         margins = [
-            keep.tile([P, PACK, HALF], F32, name=f"margin{h}", tag=f"wv_stage{h}", align_bytes=64) for h in range(2)
+            keep.tile([P, PACK, HALF], F32, name=f"margin{h}") for h in range(2)
         ]
         hinge_h0 = keep.tile([P, PACK, HALF], F32, name="hinge_h0", tag="hinge_stage", align_bytes=64)
+
+        hinge_h1 = keep.tile([P, PACK, HALF], F32, name="hinge_h1")
+        hinges = [hinge_h0, hinge_h1]
+        wv_grouped = []
+
+        def round_wv(q):
+            if q % 2 == 0:
+                wv_grouped.append(
+                    keep.tile([P, D // 2, PACK], BF16, name=f"wv_grouped{q // 2}", tag=f"wv_stage{q // 2}", align_bytes=64)
+                )
+            cols = slice(q % 2 * P, (q % 2 + 1) * P)
+            nc.scalar.copy(out=by_word(wv_grouped[q // 2][:, cols, :]), in_=by_plane(wv_raw[q // 2][:, :, cols]))
 
         def vector_weight(t):
             nc.vector.scalar_tensor_tensor(
@@ -196,6 +208,9 @@ def tile_attend_gml_sqh_kernel(tc, xT, wd, wv, y, cw, rw, offs, out):
         vector_weight(1)
         for h in range(2):
             half = slice(h * HALF, (h + 1) * HALF)
+            if h == 1:
+                round_wv(0)
+                round_wv(1)
             for u in range(2):
                 pair = slice(2 * u, 2 * u + 2)
                 a_bank = psum.tile([P, 2, HALF], F32, name=f"a_bank{2 * h + u}")
@@ -204,26 +219,7 @@ def tile_attend_gml_sqh_kernel(tc, xT, wd, wv, y, cw, rw, offs, out):
                 if h == 1 and u == 1:
                     vector_weight(2)
                 nc.vector.tensor_tensor(out=margins[h][:, pair, :], in0=a_bank[:], in1=y_planes[:, pair, half], op=MULT)
-                if h == 0:
-                    relu(hinge_h0[:, pair, :], margins[h][:, pair, :])
-
-        wv_grouped = []
-
-        def round_wv(q):
-            if q % 2 == 0:
-                wv_grouped.append(
-                    keep.tile([P, D // 2, PACK], BF16, name=f"wv_grouped{q // 2}", tag=f"wv_stage{q // 2}", align_bytes=64)
-                )
-            cols = slice(q % 2 * P, (q % 2 + 1) * P)
-            nc.scalar.copy(out=by_word(wv_grouped[q // 2][:, cols, :]), in_=by_plane(wv_raw[q // 2][:, :, cols]))
-
-        round_wv(0)
-        round_wv(1)
-        hinge_h1 = keep.tile([P, PACK, HALF], F32, name="hinge_h1", tag="late_stage0", align_bytes=64)
-        for u in range(2):
-            relu(hinge_h1[:, 2 * u : 2 * u + 2, :], margins[1][:, 2 * u : 2 * u + 2, :])
-        round_wv(2)
-        round_wv(3)
+                relu(hinges[h][:, pair, :], margins[h][:, pair, :])
 
         g_halves = [keep.tile([P, HALF, PACK], BF16, name=f"g_half{h}", align_bytes=64) for h in range(2)]
 
@@ -246,8 +242,10 @@ def tile_attend_gml_sqh_kernel(tc, xT, wd, wv, y, cw, rw, offs, out):
             second_product(early_bank, wv_codes0, wv_scales[0], q, 0)
             early.append(keep.tile([P, HALF], F32, name=f"early{q}"))
             nc.scalar.copy(out=early[q][:], in_=early_bank[:, HALF:N])
+        round_wv(2)
+        round_wv(3)
         make_g(1, hinge_h1)
-        wv_codes1 = keep.tile([P, D // 2], U32, name="wv_codes1", tag="late_stage0", align_bytes=64)
+        wv_codes1 = keep.tile([P, D // 2], U32, name="wv_codes1", align_bytes=64)
         quantize_wv(1, wv_codes1, wv_scales[1])
         quantize_g(1, g_halves[1])
         for q in range(2):

@@ -32,7 +32,7 @@ def tile_attend_gml_sqh_kernel(tc, xT, wd, wv, y, cw, rw, offs, out):
 
         offsets = keep.tile([P, N // 16], U16, name="offsets")
         x_planes = [keep.tile([P, T], F32, name=f"x_plane{t}") for t in range(PACK)]
-        wd_raw = keep.tile([P, PACK, V], F32, name="wd_raw")
+        wd_raw = keep.tile([P, PACK, V], F32, name="wd_raw", tag="wd_load", align_bytes=64)
         wv_raw = [
             keep.tile([P, PACK, D // 2], F32, name=f"wv_raw{u}") for u in range(2)
         ]
@@ -95,7 +95,7 @@ def tile_attend_gml_sqh_kernel(tc, xT, wd, wv, y, cw, rw, offs, out):
         x_grouped = keep.tile([P, N, PACK], BF16, name="x_grouped", align_bytes=64)
         wd_codes = keep.tile([P, V], U32, name="wd_codes", align_bytes=64)
         wd_scales = keep.tile([P, V], U8, name="wd_scales", align_bytes=64)
-        x_codes = keep.tile([P, N], U32, name="x_codes", align_bytes=64)
+        x_codes = [keep.tile([P, HALF], U32, name="x_codes0", align_bytes=64)]
         x_scales = keep.tile([P, N], U8, name="x_scales", align_bytes=64)
 
         for t in range(PACK - 1):
@@ -105,14 +105,16 @@ def tile_attend_gml_sqh_kernel(tc, xT, wd, wv, y, cw, rw, offs, out):
                 out=x_grouped[:, h * HALF : (h + 1) * HALF, PACK - 1],
                 in_=x_planes[PACK - 1][:].indirect(offsets[:, h * HALF // 16 : (h + 1) * HALF // 16]),
             )
-        for h in range(2):
+
+        def quantize_x(h):
             half = slice(h * HALF, (h + 1) * HALF)
             nc.vector.quantize_mx(
-                out=x_codes[:, half].bitcast(E4),
+                out=x_codes[h][:].bitcast(E4),
                 scales=x_scales[:, half],
                 in_=x_grouped[:, half, :].rearrange("p n t -> p (n t)"),
             )
 
+        quantize_x(0)
         nc.vector.tensor_copy(out=wd_to[:, :, :, 0:2], in_=wd_from[:, :, :, 0:2])
         nc.vector.tensor_copy(out=wd_to[:, 0:WD_EXTRA, :, 2:4], in_=wd_from[:, 0:WD_EXTRA, :, 2:4])
         nc.scalar.copy(out=wd_to[:, WD_EXTRA:P, :, 2:4], in_=wd_from[:, WD_EXTRA:P, :, 2:4])
@@ -124,13 +126,16 @@ def tile_attend_gml_sqh_kernel(tc, xT, wd, wv, y, cw, rw, offs, out):
                 in_=wd_grouped[:, 2 * u : 2 * u + 2].rearrange("p t m j -> p (t m j)"),
             )
 
-        def first_product(bank, t, cols):
+        x_codes.append(keep.tile([P, HALF], U32, name="x_codes1", tag="wd_load", align_bytes=64))
+        quantize_x(1)
+
+        def first_product(bank, t, h):
             nc.tensor.matmul_mx(
                 out=bank,
                 lhsT=wd_codes[:, t * P : (t + 1) * P].bitcast(E4),
                 lhsT_scale=wd_scales[:, t * P : (t + 1) * P],
-                rhs=x_codes[:, cols].bitcast(E4),
-                rhs_scale=x_scales[:, cols],
+                rhs=x_codes[h][:].bitcast(E4),
+                rhs_scale=x_scales[:, h * HALF : (h + 1) * HALF],
                 start=True,
                 stop=True,
             )
@@ -174,7 +179,7 @@ def tile_attend_gml_sqh_kernel(tc, xT, wd, wv, y, cw, rw, offs, out):
         margins = [
             keep.tile([P, PACK, HALF], F32, name=f"margin{h}") for h in range(2)
         ]
-        hinge_h0 = keep.tile([P, PACK, HALF], F32, name="hinge_h0", tag="hinge_stage", align_bytes=64)
+        hinge_h0 = keep.tile([P, PACK, HALF], F32, name="hinge_h0")
 
         hinge_h1 = keep.tile([P, PACK, HALF], F32, name="hinge_h1")
         hinges = [hinge_h0, hinge_h1]
@@ -215,7 +220,7 @@ def tile_attend_gml_sqh_kernel(tc, xT, wd, wv, y, cw, rw, offs, out):
                 pair = slice(2 * u, 2 * u + 2)
                 a_bank = psum.tile([P, 2, HALF], F32, name=f"a_bank{2 * h + u}")
                 for e in range(2):
-                    first_product(a_bank[:, e, :], 2 * u + e, half)
+                    first_product(a_bank[:, e, :], 2 * u + e, h)
                 if h == 1 and u == 1:
                     vector_weight(2)
                 nc.vector.tensor_tensor(out=margins[h][:, pair, :], in0=a_bank[:], in1=y_planes[:, pair, half], op=MULT)
@@ -232,7 +237,7 @@ def tile_attend_gml_sqh_kernel(tc, xT, wd, wv, y, cw, rw, offs, out):
             )
 
         make_g(0, hinge_h0)
-        wv_codes0 = keep.tile([P, D // 2], U32, name="wv_codes0", tag="hinge_stage", align_bytes=64)
+        wv_codes0 = keep.tile([P, D // 2], U32, name="wv_codes0", align_bytes=64)
         wv_scales = [keep.tile([P, D // 2], U8, name=f"wv_scales{u}", align_bytes=64) for u in range(2)]
         quantize_wv(0, wv_codes0, wv_scales[0])
         quantize_g(0, g_halves[0])

@@ -61,8 +61,7 @@ def tile_attend_gml_sqh_kernel(tc, xT, wd, wv, y, cw, rw, offs, out):
         identity = keep.tile([P, P], F32, name="identity")
         make_identity(nc, identity[:])
         for q in range(PACK):
-            engine = nc.vector if q < 2 else nc.gpsimd
-            engine.memset(windows[q][:].bitcast(U32), 0)
+            nc.vector.memset(windows[q][:].bitcast(U32), 0)
         nc.vector.memset(g_codes[:, 0:HALF], 0)
         nc.vector.memset(g_scales[:, 0:HALF].bitcast(U32), 0)
 

@@ -39,7 +39,7 @@ def tile_attend_gml_sqh_kernel(tc, xT, wd, wv, y, cw, rw, offs, out):
         y_planes = keep.tile([P, PACK, N], F32, name="y_planes")
         cw_raw = keep.tile([P, PACK], F32, name="cw_raw")
         rw_raw = keep.tile([P, PACK], F32, name="rw_raw")
-        windows = [keep.tile([P, T], F32, name=f"window{q}") for q in range(PACK)]
+        windows = [keep.tile([P, T], F32, name=f"window{q}") for q in range(PACK - 1)]
 
         x_rows = xT.rearrange("(p t) w -> p t w", t=PACK)
         y_rows = y.rearrange("(p t) n -> p t n", t=PACK)
@@ -60,7 +60,7 @@ def tile_attend_gml_sqh_kernel(tc, xT, wd, wv, y, cw, rw, offs, out):
         g_scales = keep.tile([P, HALF + N], U8, name="g_scales", align_bytes=64)
         identity = keep.tile([P, P], F32, name="identity")
         make_identity(nc, identity[:])
-        for q in range(PACK):
+        for q in range(PACK - 1):
             nc.vector.memset(windows[q][:].bitcast(U32), 0)
         nc.vector.memset(g_codes[:, 0:HALF], 0)
         nc.vector.memset(g_scales[:, 0:HALF].bitcast(U32), 0)
@@ -252,6 +252,8 @@ def tile_attend_gml_sqh_kernel(tc, xT, wd, wv, y, cw, rw, offs, out):
         wv_codes1 = keep.tile([P, D // 2], U32, name="wv_codes1", align_bytes=64)
         quantize_wv(1, wv_codes1, wv_scales[1])
         quantize_g(1, g_halves[1])
+        windows.append(keep.tile([P, T], F32, name="window3", tag="g_half1", align_bytes=64))
+        nc.gpsimd.memset(windows[PACK - 1][:].bitcast(U32), 0)
         for q in range(2):
             scatter(q, early[q], 0, HALF)
         wv_codes = [wv_codes0, wv_codes1]

@@ -37,17 +37,18 @@ def tile_attend_gml_sqh_kernel(tc, xT, wd, wv, y, cw, rw, offs, out):
             keep.tile([P, PACK, D // 2], F32, name=f"wv_raw{u}") for u in range(2)
         ]
         y_planes = keep.tile([P, PACK, N], F32, name="y_planes")
-        cw_raw = keep.tile([P, PACK], F32, name="cw_raw")
+        factor_rows = keep.tile([P, N], F32, name="factor_rows")
         rw_raw = keep.tile([P, PACK], F32, name="rw_raw")
         windows = [keep.tile([P, T], F32, name=f"window{q}") for q in range(PACK - 1)]
 
         x_rows = xT.rearrange("(p t) w -> p t w", t=PACK)
         y_rows = y.rearrange("(p t) n -> p t n", t=PACK)
         wv_rows = wv.rearrange("(p j) c -> p j c", j=PACK)
+        nc.vector.memset(factor_rows[:].bitcast(U32), 0)
         nc.sync.dma_start(out=x_planes[0][:], in_=x_rows[:, 0, :])
         nc.sync.dma_start(offsets[:], offs)
-        nc.scalar.dma_start(out=cw_raw[:], in_=cw.rearrange("(p t) o -> p (t o)", t=PACK))
-        nc.scalar.dma_start(out=rw_raw[:], in_=rw[0:1, :].rearrange("o (p j) -> (o p) j", j=PACK))
+        nc.sync.dma_start(out=factor_rows[0:1, :], in_=cw.rearrange("v o -> o v"))
+        nc.sync.dma_start(out=factor_rows[1:2, :], in_=rw[0:1, :])
         for t in range(1, PACK):
             nc.sync.dma_start(out=x_planes[t][:], in_=x_rows[:, t, :])
         nc.sync.dma_start(out=wd_raw[:], in_=wd.rearrange("(p j) c -> p j c", j=PACK))
@@ -66,7 +67,11 @@ def tile_attend_gml_sqh_kernel(tc, xT, wd, wv, y, cw, rw, offs, out):
         nc.vector.memset(g_scales[:, 0:HALF].bitcast(U32), 0)
 
         neg_cw = keep.tile([P, PACK], F32, name="neg_cw")
-        nc.vector.tensor_scalar(out=neg_cw[:], in0=cw_raw[:], scalar1=-1.0, scalar2=None, op0=MULT)
+        factor_bank = psum.tile([P, PACK, P], F32, name="factor_bank")
+        for t in range(PACK):
+            nc.tensor.transpose(factor_bank[:, t, :], factor_rows[:, t:N:PACK], identity[:])
+        nc.scalar.activation(out=neg_cw[:], in_=factor_bank[:, :, 0], func=COPY, scale=-1.0)
+        nc.scalar.copy(out=rw_raw[:], in_=factor_bank[:, :, 1])
         rw_bank = psum.tile([P, PACK, P], F32, name="rw_bank")
         for j in range(PACK):
             nc.tensor.transpose(rw_bank[:, j, :], rw_raw[:, j : j + 1].to_broadcast([P, P]), identity[:])

@@ -71,24 +71,27 @@ def tile_attend_gml_sqh_kernel(tc, xT, wd, wv, y, cw, rw, offs, out):
         for t in range(PACK):
             nc.tensor.transpose(factor_bank[:, t, :], factor_rows[:, t:N:PACK], identity[:])
         nc.scalar.activation(out=neg_cw[:], in_=factor_bank[:, :, 0], func=COPY, scale=-1.0)
-        nc.scalar.copy(out=rw_raw[:], in_=factor_bank[:, :, 1])
+        rw_turn = psum.tile([P, PACK, P], F32, name="early_bank0")
+        for j in range(PACK):
+            nc.tensor.transpose(rw_turn[:, j, :], factor_rows[:, j * P : (j + 1) * P], identity[:])
+        nc.scalar.copy(out=rw_raw[:], in_=rw_turn[:, :, 1])
         rw_bank = psum.tile([P, PACK, P], F32, name="rw_bank")
         for j in range(PACK):
             nc.tensor.transpose(rw_bank[:, j, :], rw_raw[:, j : j + 1].to_broadcast([P, P]), identity[:])
-        rw_all = rw_bank[:].rearrange("p j n -> p n j")
+        rw_all = rw_bank[:].rearrange("p j n -> p (j n)")
         outer = keep.tile([P, PACK, HALF], F32, name="outer")
         for t in range(PACK):
             nc.scalar.activation(
-                out=outer[:, t, :].rearrange("p (n j) -> p n j", j=PACK),
-                in_=rw_all[:, 0 : HALF // PACK, :],
+                out=outer[:, t, :],
+                in_=rw_all[:, 0:HALF],
                 func=COPY,
                 scale=neg_cw[:, t : t + 1],
             )
 
         outer_last = keep.tile([P, HALF], F32, name="outer_last")
         nc.scalar.activation(
-            out=outer_last[:].rearrange("p (n j) -> p n j", j=PACK),
-            in_=rw_all[:, HALF // PACK : N // PACK, :],
+            out=outer_last[:],
+            in_=rw_all[:, HALF:N],
             func=COPY,
             scale=neg_cw[:, PACK - 1 : PACK],
         )
@@ -199,10 +202,10 @@ def tile_attend_gml_sqh_kernel(tc, xT, wd, wv, y, cw, rw, offs, out):
 
         def vector_weight(t):
             nc.vector.scalar_tensor_tensor(
-                out=weight[:, t, HALF:N].rearrange("p (n j) -> p n j", j=PACK),
-                in0=y_planes[:, t, HALF:N].rearrange("p (n j) -> p n j", j=PACK),
+                out=weight[:, t, HALF:N],
+                in0=y_planes[:, t, HALF:N],
                 scalar=neg_cw[:, t : t + 1],
-                in1=rw_all[:, HALF // PACK : N // PACK, :],
+                in1=rw_all[:, HALF:N],
                 op0=MULT,
                 op1=MULT,
             )
@@ -270,8 +273,4 @@ def tile_attend_gml_sqh_kernel(tc, xT, wd, wv, y, cw, rw, offs, out):
             nc.scalar.copy(out=dx[:], in_=dx_bank[:, first:N])
             scatter(q, dx, first, N)
             rows = slice(q * P, (q + 1) * P)
-            if q < PACK - 1:
-                nc.sync.dma_start(out=out[rows, :], in_=windows[q][:])
-            else:
-                nc.sync.dma_start(out=out[rows, 0 : T // 2], in_=windows[q][:, 0 : T // 2])
-                nc.scalar.dma_start(out=out[rows, T // 2 : T], in_=windows[q][:, T // 2 : T])
+            nc.sync.dma_start(out=out[rows, :], in_=windows[q][:])

@@ -44,11 +44,11 @@ def tile_attend_gml_sqh_kernel(tc, xT, wd, wv, y, cw, rw, offs, out):
         x_rows = xT.rearrange("(p t) w -> p t w", t=PACK)
         y_rows = y.rearrange("(p t) n -> p t n", t=PACK)
         wv_rows = wv.rearrange("(p j) c -> p j c", j=PACK)
-        nc.vector.memset(factor_rows[:].bitcast(U32), 0)
+        nc.vector.memset(factor_rows[0 : P - 2, :].bitcast(U32), 0)
         nc.sync.dma_start(out=x_planes[0][:], in_=x_rows[:, 0, :])
         nc.sync.dma_start(offsets[:], offs)
-        nc.sync.dma_start(out=factor_rows[0:1, :], in_=cw.rearrange("v o -> o v"))
-        nc.sync.dma_start(out=factor_rows[1:2, :], in_=rw[0:1, :])
+        nc.scalar.dma_start(out=factor_rows[P - 2 : P - 1, :], in_=cw.rearrange("v o -> o v"))
+        nc.scalar.dma_start(out=factor_rows[P - 1 : P, :], in_=rw[0:1, :])
         for t in range(1, PACK):
             nc.sync.dma_start(out=x_planes[t][:], in_=x_rows[:, t, :])
         nc.sync.dma_start(out=wd_raw[:], in_=wd.rearrange("(p j) c -> p j c", j=PACK))
@@ -70,11 +70,11 @@ def tile_attend_gml_sqh_kernel(tc, xT, wd, wv, y, cw, rw, offs, out):
         factor_bank = psum.tile([P, PACK, P], F32, name="factor_bank")
         for t in range(PACK):
             nc.tensor.transpose(factor_bank[:, t, :], factor_rows[:, t:N:PACK], identity[:])
-        nc.scalar.activation(out=neg_cw[:], in_=factor_bank[:, :, 0], func=COPY, scale=-1.0)
+        nc.scalar.activation(out=neg_cw[:], in_=factor_bank[:, :, P - 2], func=COPY, scale=-1.0)
         rw_turn = psum.tile([P, PACK, P], F32, name="early_bank0")
         for j in range(PACK):
             nc.tensor.transpose(rw_turn[:, j, :], factor_rows[:, j * P : (j + 1) * P], identity[:])
-        nc.scalar.copy(out=rw_raw[:], in_=rw_turn[:, :, 1])
+        nc.scalar.copy(out=rw_raw[:], in_=rw_turn[:, :, P - 1])
         rw_bank = psum.tile([P, PACK, P], F32, name="rw_bank")
         for j in range(PACK):
             nc.tensor.transpose(rw_bank[:, j, :], rw_raw[:, j : j + 1].to_broadcast([P, P]), identity[:])

@@ -57,14 +57,12 @@ def tile_attend_gml_sqh_kernel(tc, xT, wd, wv, y, cw, rw, offs, out):
         for u in range(2):
             nc.sync.dma_start(out=wv_raw[u][:], in_=wv_rows[:, :, u * (D // 2) : (u + 1) * (D // 2)])
 
-        g_codes = keep.tile([P, HALF + N], U32, name="g_codes", align_bytes=64)
-        g_scales = keep.tile([P, HALF + N], U8, name="g_scales", align_bytes=64)
+        g_codes = keep.tile([P, N], U32, name="g_codes", align_bytes=64)
+        g_scales = keep.tile([P, N], U8, name="g_scales", align_bytes=64)
         identity = keep.tile([P, P], F32, name="identity")
         make_identity(nc, identity[:])
         for q in range(PACK - 1):
             nc.vector.memset(windows[q][:].bitcast(U32), 0)
-        nc.vector.memset(g_codes[:, 0:HALF], 0)
-        nc.vector.memset(g_scales[:, 0:HALF].bitcast(U32), 0)
 
         neg_cw = keep.tile([P, PACK], F32, name="neg_cw")
         factor_bank = psum.tile([P, PACK, P], F32, name="factor_bank")
@@ -162,25 +160,25 @@ def tile_attend_gml_sqh_kernel(tc, xT, wd, wv, y, cw, rw, offs, out):
             )
 
         def quantize_g(h, grouped):
-            to = slice((h + 1) * HALF, (h + 2) * HALF)
+            to = slice(h * HALF, (h + 1) * HALF)
             nc.vector.quantize_mx(
                 out=g_codes[:, to].bitcast(E5), scales=g_scales[:, to], in_=grouped[:].rearrange("p n t -> p (n t)")
             )
 
-        def second_product(bank, codes, scales, q, first):
+        def second_product(bank, codes, scales, q, first, last):
             cols = slice(q % 2 * P, (q % 2 + 1) * P)
             nc.tensor.matmul_mx(
-                out=bank[:],
+                out=bank,
                 lhsT=codes[:, cols].bitcast(E4),
                 lhsT_scale=scales[:, cols],
-                rhs=g_codes[:, first : first + N].bitcast(E5),
-                rhs_scale=g_scales[:, first : first + N],
+                rhs=g_codes[:, first:last].bitcast(E5),
+                rhs_scale=g_scales[:, first:last],
                 start=True,
                 stop=True,
             )
 
-        def scatter(q, values, first, last):
-            nc.vector.tensor_copy(out=windows[q][:].indirect(offsets[:, first // 16 : last // 16]), in_=values[:])
+        def listed(q, first, last):
+            return windows[q][:].indirect(offsets[:, first // 16 : last // 16])
 
         weight = keep.tile([P, PACK, N], F32, name="weight", tag="wd_stage", align_bytes=64)
         margins = [
@@ -248,29 +246,30 @@ def tile_attend_gml_sqh_kernel(tc, xT, wd, wv, y, cw, rw, offs, out):
         wv_scales = [keep.tile([P, D // 2], U8, name=f"wv_scales{u}", align_bytes=64) for u in range(2)]
         quantize_wv(0, wv_codes0, wv_scales[0])
         quantize_g(0, g_halves[0])
-        early = []
-        for q in range(2):
-            early_bank = psum.tile([P, N], F32, name=f"early_bank{q}")
-            second_product(early_bank, wv_codes0, wv_scales[0], q, 0)
-            early.append(keep.tile([P, HALF], F32, name=f"early{q}"))
-            nc.scalar.copy(out=early[q][:], in_=early_bank[:, HALF:N])
+        dx = [keep.tile([P, N], F32, name=f"dx{q}") for q in range(PACK)]
+        early_bank = psum.tile([P, HALF], F32, name="early_bank0")
+        second_product(early_bank[:], wv_codes0, wv_scales[0], 0, 0, HALF)
         round_wv(2)
         round_wv(3)
+        nc.scalar.copy(out=dx[0][:, 0:HALF], in_=early_bank[:])
+        nc.scalar.activation(out=listed(0, 0, HALF), in_=dx[0][:, 0:HALF], func=COPY)
         make_g(1, hinge_h1)
         wv_codes1 = keep.tile([P, D // 2], U32, name="wv_codes1", align_bytes=64)
         quantize_wv(1, wv_codes1, wv_scales[1])
         quantize_g(1, g_halves[1])
         windows.append(keep.tile([P, T], F32, name="window3", tag="g_half1", align_bytes=64))
         nc.gpsimd.memset(windows[PACK - 1][:].bitcast(U32), 0)
-        for q in range(2):
-            scatter(q, early[q], 0, HALF)
         wv_codes = [wv_codes0, wv_codes1]
         for q in range(PACK):
-            first = HALF if q < 2 else 0
-            dx_bank = psum.tile([P, N], F32, name=f"a_bank{q}")
-            second_product(dx_bank, wv_codes[q // 2], wv_scales[q // 2], q, HALF)
-            dx = keep.tile([P, N - first], F32, name=f"dx{q}")
-            nc.scalar.copy(out=dx[:], in_=dx_bank[:, first:N])
-            scatter(q, dx, first, N)
+            first = HALF if q == 0 else 0
+            dx_bank = psum.tile([P, N - first], F32, name=f"a_bank{q}")
+            second_product(dx_bank[:], wv_codes[q // 2], wv_scales[q // 2], q, first, N)
+            if q % 2 == 0:
+                nc.scalar.copy(out=dx[q][:, first:N], in_=dx_bank[:])
+                for at in range(first, N, HALF):
+                    nc.scalar.activation(out=listed(q, at, at + HALF), in_=dx[q][:, at : at + HALF], func=COPY)
+            else:
+                nc.vector.tensor_copy(out=dx[q][:], in_=dx_bank[:])
+                nc.vector.tensor_copy(out=listed(q, 0, N), in_=dx[q][:])
             rows = slice(q * P, (q + 1) * P)
             nc.sync.dma_start(out=out[rows, :], in_=windows[q][:])

@@ -29,6 +29,8 @@ def tile_attend_gml_sqh_kernel(tc, xT, wd, wv, y, cw, rw, offs, out):
     with ExitStack() as ctx:
         keep = ctx.enter_context(tc.tile_pool(name="keep", bufs=1))
         psum = ctx.enter_context(tc.psum_pool(name="psum", bufs=1))
+        staged = ctx.enter_context(tc.tile_pool(name="staged", bufs=1))
+        late = ctx.enter_context(tc.tile_pool(name="late", bufs=1))
 
         offsets = keep.tile([P, N // 16], U16, name="offsets")
         x_planes = [keep.tile([P, T], F32, name=f"x_plane{t}") for t in range(PACK)]
@@ -154,49 +156,34 @@ def tile_attend_gml_sqh_kernel(tc, xT, wd, wv, y, cw, rw, offs, out):
         def by_word(words):
             return words.rearrange("p (c i) t -> p c t i", i=4)
 
-        def quantize_wv(u, codes, scales):
+        def quantize_wv(first, last, grouped):
+            cols = slice(first * P, last * P)
             nc.vector.quantize_mx(
-                out=codes[:].bitcast(E4), scales=scales[:], in_=wv_grouped[u][:].rearrange("p c j -> p (c j)")
+                out=wv_codes[:, cols].bitcast(E4),
+                scales=wv_scales[:, cols],
+                in_=grouped[:].rearrange("p c j -> p (c j)"),
             )
 
-        def quantize_g(h, grouped):
+        def quantize_g(h):
             to = slice(h * HALF, (h + 1) * HALF)
             nc.vector.quantize_mx(
-                out=g_codes[:, to].bitcast(E5), scales=g_scales[:, to], in_=grouped[:].rearrange("p n t -> p (n t)")
+                out=g_codes[:, to].bitcast(E5),
+                scales=g_scales[:, to],
+                in_=g_halves[h][:].rearrange("p n t -> p (n t)"),
             )
 
-        def second_product(bank, codes, scales, q, first, last):
+        def round_wv(q, engine_copy, to):
             cols = slice(q % 2 * P, (q % 2 + 1) * P)
-            nc.tensor.matmul_mx(
-                out=bank,
-                lhsT=codes[:, cols].bitcast(E4),
-                lhsT_scale=scales[:, cols],
-                rhs=g_codes[:, first:last].bitcast(E5),
-                rhs_scale=g_scales[:, first:last],
-                start=True,
-                stop=True,
-            )
-
-        def listed(q, first, last):
-            return windows[q][:].indirect(offsets[:, first // 16 : last // 16])
+            engine_copy(out=by_word(to), in_=by_plane(wv_raw[q // 2][:, :, cols]))
 
         weight = keep.tile([P, PACK, N], F32, name="weight", tag="wd_stage", align_bytes=64)
-        margins = [
-            keep.tile([P, PACK, HALF], F32, name=f"margin{h}") for h in range(2)
-        ]
-        hinge_h0 = keep.tile([P, PACK, HALF], F32, name="hinge_h0")
-
-        hinge_h1 = keep.tile([P, PACK, HALF], F32, name="hinge_h1")
-        hinges = [hinge_h0, hinge_h1]
-        wv_grouped = []
-
-        def round_wv(q):
-            if q % 2 == 0:
-                wv_grouped.append(
-                    keep.tile([P, D // 2, PACK], BF16, name=f"wv_grouped{q // 2}", tag=f"wv_stage{q // 2}", align_bytes=64)
-                )
-            cols = slice(q % 2 * P, (q % 2 + 1) * P)
-            nc.scalar.copy(out=by_word(wv_grouped[q // 2][:, cols, :]), in_=by_plane(wv_raw[q // 2][:, :, cols]))
+        margins = [keep.tile([P, PACK, HALF], F32, name=f"margin{h}") for h in range(2)]
+        hinges = [keep.tile([P, PACK, HALF], F32, name=f"hinge{h}", align_bytes=64) for h in range(2)]
+        wv_codes = keep.tile([P, D], U32, name="wv_codes", align_bytes=64)
+        wv_scales = keep.tile([P, D], U8, name="wv_scales", align_bytes=64)
+        wv_first = keep.tile([P, P, PACK], BF16, name="wv_first", align_bytes=64)
+        wv_middle = late.tile([P, 2 * P, PACK], BF16, name="wv_middle", align_bytes=64, offset=0)
+        g_halves = [keep.tile([P, HALF, PACK], BF16, name="g_half0", align_bytes=64)]
 
         def vector_weight(t):
             nc.vector.scalar_tensor_tensor(
@@ -219,8 +206,7 @@ def tile_attend_gml_sqh_kernel(tc, xT, wd, wv, y, cw, rw, offs, out):
         for h in range(2):
             half = slice(h * HALF, (h + 1) * HALF)
             if h == 1:
-                round_wv(0)
-                round_wv(1)
+                round_wv(0, nc.scalar.copy, wv_first[:])
             for u in range(2):
                 pair = slice(2 * u, 2 * u + 2)
                 a_bank = psum.tile([P, 2, HALF], F32, name=f"a_bank{2 * h + u}")
@@ -231,45 +217,89 @@ def tile_attend_gml_sqh_kernel(tc, xT, wd, wv, y, cw, rw, offs, out):
                 nc.vector.tensor_tensor(out=margins[h][:, pair, :], in0=a_bank[:], in1=y_planes[:, pair, half], op=MULT)
                 relu(hinges[h][:, pair, :], margins[h][:, pair, :])
 
-        g_halves = [keep.tile([P, HALF, PACK], BF16, name=f"g_half{h}", align_bytes=64) for h in range(2)]
-
-        def make_g(h, hinge):
+        def make_g(h):
             nc.vector.tensor_tensor(
                 out=by_word(g_halves[h][:]),
-                in0=by_plane(hinge[:]),
+                in0=by_plane(hinges[h][:]),
                 in1=by_plane(weight[:, :, h * HALF : (h + 1) * HALF]),
                 op=MULT,
             )
 
-        make_g(0, hinge_h0)
-        wv_codes0 = keep.tile([P, D // 2], U32, name="wv_codes0", align_bytes=64)
-        wv_scales = [keep.tile([P, D // 2], U8, name=f"wv_scales{u}", align_bytes=64) for u in range(2)]
-        quantize_wv(0, wv_codes0, wv_scales[0])
-        quantize_g(0, g_halves[0])
-        dx = [keep.tile([P, N], F32, name=f"dx{q}") for q in range(PACK)]
-        early_bank = psum.tile([P, HALF], F32, name="early_bank0")
-        second_product(early_bank[:], wv_codes0, wv_scales[0], 0, 0, HALF)
-        round_wv(2)
-        round_wv(3)
-        nc.scalar.copy(out=dx[0][:, 0:HALF], in_=early_bank[:])
-        nc.scalar.activation(out=listed(0, 0, HALF), in_=dx[0][:, 0:HALF], func=COPY)
-        make_g(1, hinge_h1)
-        wv_codes1 = keep.tile([P, D // 2], U32, name="wv_codes1", align_bytes=64)
-        quantize_wv(1, wv_codes1, wv_scales[1])
-        quantize_g(1, g_halves[1])
-        windows.append(keep.tile([P, T], F32, name="window3", tag="g_half1", align_bytes=64))
-        nc.gpsimd.memset(windows[PACK - 1][:].bitcast(U32), 0)
-        wv_codes = [wv_codes0, wv_codes1]
-        for q in range(PACK):
-            first = HALF if q == 0 else 0
-            dx_bank = psum.tile([P, N - first], F32, name=f"a_bank{q}")
-            second_product(dx_bank[:], wv_codes[q // 2], wv_scales[q // 2], q, first, N)
-            if q % 2 == 0:
-                nc.scalar.copy(out=dx[q][:, first:N], in_=dx_bank[:])
-                for at in range(first, N, HALF):
-                    nc.scalar.activation(out=listed(q, at, at + HALF), in_=dx[q][:, at : at + HALF], func=COPY)
+        bank_names = {(0, 0): "early_bank0", (1, 0): "early_bank1", (0, 1): "a_bank0", (1, 1): "a_bank1",
+                      (2, 0): "a_bank2", (3, 0): "a_bank3", (2, 1): "factor_bank", (3, 1): "rw_bank"}
+        banks = {}
+        shared_at = {(1, 0): 512, (2, 0): 0, (3, 0): 1024}
+        dx = {}
+
+        def product(q, h):
+            banks[q, h] = psum.tile([P, HALF], F32, name=bank_names[q, h])
+            cols = slice(q * P, (q + 1) * P)
+            half = slice(h * HALF, (h + 1) * HALF)
+            nc.tensor.matmul_mx(
+                out=banks[q, h][:],
+                lhsT=wv_codes[:, cols].bitcast(E4),
+                lhsT_scale=wv_scales[:, cols],
+                rhs=g_codes[:, half].bitcast(E5),
+                rhs_scale=g_scales[:, half],
+                start=True,
+                stop=True,
+            )
+
+        def fetch(q, h, engine_copy):
+            if (q, h) in shared_at:
+                dx[q, h] = staged.tile([P, HALF], F32, name=f"dx{q}{h}", offset=shared_at[q, h])
             else:
-                nc.vector.tensor_copy(out=dx[q][:], in_=dx_bank[:])
-                nc.vector.tensor_copy(out=listed(q, 0, N), in_=dx[q][:])
-            rows = slice(q * P, (q + 1) * P)
-            nc.sync.dma_start(out=out[rows, :], in_=windows[q][:])
+                dx[q, h] = keep.tile([P, HALF], F32, name=f"dx{q}{h}")
+            engine_copy(out=dx[q, h][:], in_=banks[q, h][:])
+
+        def listed(q, h):
+            return windows[q][:].indirect(offsets[:, h * HALF // 16 : (h + 1) * HALF // 16])
+
+        def vector_scatter(q, h):
+            nc.vector.tensor_copy(out=listed(q, h), in_=dx[q, h][:])
+
+        def scalar_scatter(q, h):
+            nc.scalar.activation(out=listed(q, h), in_=dx[q, h][:], func=COPY)
+
+        def store(q):
+            nc.sync.dma_start(out=out[q * P : (q + 1) * P, :], in_=windows[q][:])
+
+        for q in (1, 2):
+            round_wv(q, nc.scalar.copy, wv_middle[:, (q - 1) * P : q * P, :])
+        make_g(0)
+        quantize_wv(0, 1, wv_first)
+        quantize_g(0)
+        product(0, 0)
+        fetch(0, 0, nc.scalar.copy)
+        scalar_scatter(0, 0)
+        g_halves.append(keep.tile([P, HALF, PACK], BF16, name="g_half1", tag="hinge0", align_bytes=64))
+        make_g(1)
+        quantize_wv(1, 3, wv_middle)
+        quantize_g(1)
+        product(1, 0)
+        product(0, 1)
+        product(1, 1)
+        wv_last = late.tile([P, P, PACK], BF16, name="wv_last", align_bytes=64, offset=0)
+        round_wv(3, nc.vector.tensor_copy, wv_last[:])
+        fetch(1, 0, nc.vector.tensor_copy)
+        quantize_wv(3, 4, wv_last)
+        windows.append(late.tile([P, T], F32, name="window3", align_bytes=64, offset=0))
+        nc.gpsimd.memset(windows[PACK - 1][:].bitcast(U32), 0)
+        scalar_scatter(1, 0)
+        for q, h in ((2, 0), (3, 0), (2, 1), (3, 1)):
+            product(q, h)
+        for q in range(2):
+            fetch(q, 1, nc.vector.tensor_copy)
+        for q in range(2):
+            vector_scatter(q, 1)
+            store(q)
+        for q in range(2, PACK):
+            fetch(q, 0, nc.scalar.copy)
+        for q in range(2, PACK):
+            scalar_scatter(q, 0)
+        for q in range(2, PACK):
+            fetch(q, 1, nc.vector.tensor_copy)
+        vector_scatter(2, 1)
+        store(2)
+        scalar_scatter(3, 1)
+        store(3)

@@ -299,7 +299,6 @@ def tile_attend_gml_sqh_kernel(tc, xT, wd, wv, y, cw, rw, offs, out):
             scalar_scatter(q, 0)
         for q in range(2, PACK):
             fetch(q, 1, nc.vector.tensor_copy)
-        vector_scatter(2, 1)
-        store(2)
-        scalar_scatter(3, 1)
-        store(3)
+        for q in range(2, PACK):
+            vector_scatter(q, 1)
+            store(q)

@@ -99,29 +99,42 @@ def tile_attend_gml_sqh_kernel(tc, xT, wd, wv, y, cw, rw, offs, out):
         wd_grouped = keep.tile([P, PACK, P, PACK], BF16, name="wd_grouped", tag="wd_stage", align_bytes=64)
         wd_to = wd_grouped[:].rearrange("p t m j -> p m j t")
         wd_from = wd_raw[:].rearrange("p j (m t) -> p m j t", t=PACK)
-        x_grouped = keep.tile([P, N, PACK], BF16, name="x_grouped", align_bytes=64)
+        x_grouped = [keep.tile([P, HALF, PACK], BF16, name=f"x_grouped{h}", align_bytes=64) for h in range(2)]
+        x_dense = keep.tile([P, 2, HALF], BF16, name="x_dense")
         wd_codes = keep.tile([P, V], U32, name="wd_codes", align_bytes=64)
         wd_scales = keep.tile([P, V], U8, name="wd_scales", align_bytes=64)
-        x_codes = [keep.tile([P, HALF], U32, name="x_codes0", align_bytes=64)]
+        x_codes = [keep.tile([P, HALF], U32, name=f"x_codes{h}", align_bytes=64) for h in range(2)]
         x_scales = keep.tile([P, N], U8, name="x_scales", align_bytes=64)
 
-        for t in range(PACK - 1):
-            nc.vector.tensor_copy(out=x_grouped[:, :, t], in_=x_planes[t][:].indirect(offsets[:]))
-        for h in range(2):
-            nc.vector.tensor_copy(
-                out=x_grouped[:, h * HALF : (h + 1) * HALF, PACK - 1],
-                in_=x_planes[PACK - 1][:].indirect(offsets[:, h * HALF // 16 : (h + 1) * HALF // 16]),
-            )
+        def picked(t, first, last):
+            return x_planes[t][:].indirect(offsets[:, first // 16 : last // 16])
+
+        for t in range(PACK):
+            nc.vector.tensor_copy(out=x_grouped[0][:, :, t], in_=picked(t, 0, HALF))
+            if t < 2:
+                nc.vector.tensor_copy(out=x_grouped[1][:, :, t], in_=picked(t, HALF, N))
+            elif t == 2:
+                nc.scalar.activation(out=x_dense[:, 0, :], in_=picked(t, HALF, N), func=COPY)
+            else:
+                for c in range(2):
+                    at = c * QUARTER
+                    nc.scalar.activation(
+                        out=x_dense[:, 1, at : at + QUARTER], in_=picked(t, HALF + at, HALF + at + QUARTER), func=COPY
+                    )
+        for c in range(2):
+            quarter = slice(c * QUARTER, (c + 1) * QUARTER)
+            nc.scalar.copy(out=x_grouped[1][:, quarter, 2:4], in_=x_dense[:, :, quarter].rearrange("p e n -> p n e"))
 
         def quantize_x(h):
             half = slice(h * HALF, (h + 1) * HALF)
             nc.vector.quantize_mx(
                 out=x_codes[h][:].bitcast(E4),
                 scales=x_scales[:, half],
-                in_=x_grouped[:, half, :].rearrange("p n t -> p (n t)"),
+                in_=x_grouped[h][:].rearrange("p n t -> p (n t)"),
             )
 
         quantize_x(0)
+        quantize_x(1)
         nc.vector.tensor_copy(out=wd_to[:, :, :, 0:2], in_=wd_from[:, :, :, 0:2])
         nc.vector.tensor_copy(out=wd_to[:, 0:WD_EXTRA, :, 2:4], in_=wd_from[:, 0:WD_EXTRA, :, 2:4])
         nc.scalar.copy(out=wd_to[:, WD_EXTRA:P, :, 2:4], in_=wd_from[:, WD_EXTRA:P, :, 2:4])
@@ -133,8 +146,6 @@ def tile_attend_gml_sqh_kernel(tc, xT, wd, wv, y, cw, rw, offs, out):
                 in_=wd_grouped[:, 2 * u : 2 * u + 2].rearrange("p t m j -> p (t m j)"),
             )
 
-        x_codes.append(keep.tile([P, HALF], U32, name="x_codes1", tag="wd_load", align_bytes=64))
-        quantize_x(1)
 
         def first_product(bank, t, h):
             nc.tensor.matmul_mx(

@@ -14,6 +14,7 @@ U8 = mybir.dt.uint8
 E4 = mybir.dt.float8_e4m3fn_x4
 E5 = mybir.dt.float8_e5m2_x4
 MULT = mybir.AluOpType.mult
+ADD = mybir.AluOpType.add
 COPY = mybir.ActivationFunctionType.Copy
 RELU = mybir.ActivationFunctionType.Relu
 
@@ -79,6 +80,9 @@ def tile_attend_gml_sqh_kernel(tc, xT, wd, wv, y, cw, rw, offs, out):
         for j in range(PACK):
             nc.tensor.transpose(rw_bank[:, j, :], rw_raw[:, j : j + 1].to_broadcast([P, P]), identity[:])
         rw_all = rw_bank[:].rearrange("p j n -> p (j n)")
+        rw_again = psum.tile([P, 2, P], F32, name="a_bank2")
+        for j in range(2):
+            nc.tensor.transpose(rw_again[:, j, :], rw_raw[:, 2 + j : 3 + j].to_broadcast([P, P]), identity[:])
         outer = keep.tile([P, PACK, HALF], F32, name="outer")
         for t in range(PACK):
             nc.scalar.activation(
@@ -99,8 +103,8 @@ def tile_attend_gml_sqh_kernel(tc, xT, wd, wv, y, cw, rw, offs, out):
         wd_grouped = keep.tile([P, PACK, P, PACK], BF16, name="wd_grouped", tag="wd_stage", align_bytes=64)
         wd_to = wd_grouped[:].rearrange("p t m j -> p m j t")
         wd_from = wd_raw[:].rearrange("p j (m t) -> p m j t", t=PACK)
-        x_grouped = [keep.tile([P, HALF, PACK], BF16, name=f"x_grouped{h}", align_bytes=64) for h in range(2)]
-        x_dense = keep.tile([P, 2, HALF], BF16, name="x_dense")
+        x_grouped = keep.tile([P, N, PACK], BF16, name="x_grouped", align_bytes=64)
+        x_dense = keep.tile([P, 2, QUARTER], BF16, name="x_dense")
         wd_codes = keep.tile([P, V], U32, name="wd_codes", align_bytes=64)
         wd_scales = keep.tile([P, V], U8, name="wd_scales", align_bytes=64)
         x_codes = [keep.tile([P, HALF], U32, name=f"x_codes{h}", align_bytes=64) for h in range(2)]
@@ -109,28 +113,20 @@ def tile_attend_gml_sqh_kernel(tc, xT, wd, wv, y, cw, rw, offs, out):
         def picked(t, first, last):
             return x_planes[t][:].indirect(offsets[:, first // 16 : last // 16])
 
+        split = N - QUARTER
         for t in range(PACK):
-            nc.vector.tensor_copy(out=x_grouped[0][:, :, t], in_=picked(t, 0, HALF))
-            if t < 2:
-                nc.vector.tensor_copy(out=x_grouped[1][:, :, t], in_=picked(t, HALF, N))
-            elif t == 2:
-                nc.scalar.activation(out=x_dense[:, 0, :], in_=picked(t, HALF, N), func=COPY)
-            else:
-                for c in range(2):
-                    at = c * QUARTER
-                    nc.scalar.activation(
-                        out=x_dense[:, 1, at : at + QUARTER], in_=picked(t, HALF + at, HALF + at + QUARTER), func=COPY
-                    )
-        for c in range(2):
-            quarter = slice(c * QUARTER, (c + 1) * QUARTER)
-            nc.scalar.copy(out=x_grouped[1][:, quarter, 2:4], in_=x_dense[:, :, quarter].rearrange("p e n -> p n e"))
+            last = N if t < 2 else split
+            nc.vector.tensor_copy(out=x_grouped[:, 0:last, t], in_=picked(t, 0, last))
+            if t >= 2:
+                nc.scalar.activation(out=x_dense[:, t - 2, :], in_=picked(t, split, N), func=COPY)
+        nc.scalar.copy(out=x_grouped[:, split:N, 2:4], in_=x_dense[:].rearrange("p e n -> p n e"))
 
         def quantize_x(h):
             half = slice(h * HALF, (h + 1) * HALF)
             nc.vector.quantize_mx(
                 out=x_codes[h][:].bitcast(E4),
                 scales=x_scales[:, half],
-                in_=x_grouped[h][:].rearrange("p n t -> p (n t)"),
+                in_=x_grouped[:, half, :].rearrange("p n t -> p (n t)"),
             )
 
         quantize_x(0)
@@ -138,14 +134,13 @@ def tile_attend_gml_sqh_kernel(tc, xT, wd, wv, y, cw, rw, offs, out):
         nc.vector.tensor_copy(out=wd_to[:, :, :, 0:2], in_=wd_from[:, :, :, 0:2])
         nc.vector.tensor_copy(out=wd_to[:, 0:WD_EXTRA, :, 2:4], in_=wd_from[:, 0:WD_EXTRA, :, 2:4])
         nc.scalar.copy(out=wd_to[:, WD_EXTRA:P, :, 2:4], in_=wd_from[:, WD_EXTRA:P, :, 2:4])
-        for u in range(2):
-            cols = slice(2 * u * P, (2 * u + 2) * P)
+        for first, last in ((0, 1), (1, 2), (2, PACK)):
+            cols = slice(first * P, last * P)
             nc.vector.quantize_mx(
                 out=wd_codes[:, cols].bitcast(E4),
                 scales=wd_scales[:, cols],
-                in_=wd_grouped[:, 2 * u : 2 * u + 2].rearrange("p t m j -> p (t m j)"),
+                in_=wd_grouped[:, first:last].rearrange("p t m j -> p (t m j)"),
             )
-
 
         def first_product(bank, t, h):
             nc.tensor.matmul_mx(
@@ -187,21 +182,25 @@ def tile_attend_gml_sqh_kernel(tc, xT, wd, wv, y, cw, rw, offs, out):
             cols = slice(q % 2 * P, (q % 2 + 1) * P)
             engine_copy(out=by_word(to), in_=by_plane(wv_raw[q // 2][:, :, cols]))
 
-        weight = keep.tile([P, PACK, N], F32, name="weight", tag="wd_stage", align_bytes=64)
-        margins = [keep.tile([P, PACK, HALF], F32, name=f"margin{h}") for h in range(2)]
+        weights = [
+            keep.tile([P, PACK, HALF], F32, name="weight_first", tag="wd_stage", align_bytes=64),
+            keep.tile([P, PACK, HALF], F32, name="weight_second", tag="wd_load", align_bytes=64),
+        ]
+        margins = [
+            [keep.tile([P, 2, HALF], F32, name="margin00"), late.tile([P, 2, HALF], F32, name="margin01", offset=1024)],
+            [keep.tile([P, 2, HALF], F32, name="margin10"), keep.tile([P, 2, HALF], F32, name="margin11")],
+        ]
         hinges = [keep.tile([P, PACK, HALF], F32, name=f"hinge{h}", align_bytes=64) for h in range(2)]
         wv_codes = keep.tile([P, D], U32, name="wv_codes", align_bytes=64)
         wv_scales = keep.tile([P, D], U8, name="wv_scales", align_bytes=64)
-        wv_first = keep.tile([P, P, PACK], BF16, name="wv_first", align_bytes=64)
-        wv_middle = late.tile([P, 2 * P, PACK], BF16, name="wv_middle", align_bytes=64, offset=0)
         g_halves = [keep.tile([P, HALF, PACK], BF16, name="g_half0", align_bytes=64)]
 
         def vector_weight(t):
             nc.vector.scalar_tensor_tensor(
-                out=weight[:, t, HALF:N],
+                out=weights[1][:, t, :],
                 in0=y_planes[:, t, HALF:N],
                 scalar=neg_cw[:, t : t + 1],
-                in1=rw_all[:, HALF:N],
+                in1=rw_all[:, HALF:N] if t < 2 else rw_again[:].rearrange("p j n -> p (j n)"),
                 op0=MULT,
                 op1=MULT,
             )
@@ -209,30 +208,31 @@ def tile_attend_gml_sqh_kernel(tc, xT, wd, wv, y, cw, rw, offs, out):
         for u in range(2):
             pair = slice(2 * u, 2 * u + 2)
             nc.gpsimd.tensor_tensor(
-                out=weight[:, pair, 0:HALF], in0=y_planes[:, pair, 0:HALF], in1=outer[:, pair, :], op=MULT
+                out=weights[0][:, pair, :], in0=y_planes[:, pair, 0:HALF], in1=outer[:, pair, :], op=MULT
             )
-        nc.gpsimd.tensor_tensor(out=weight[:, 3, HALF:N], in0=y_planes[:, 3, HALF:N], in1=outer_last[:], op=MULT)
+        nc.gpsimd.tensor_tensor(out=weights[1][:, 3, :], in0=y_planes[:, 3, HALF:N], in1=outer_last[:], op=MULT)
         vector_weight(0)
         vector_weight(1)
         for h in range(2):
             half = slice(h * HALF, (h + 1) * HALF)
             if h == 1:
+                wv_first = late.tile([P, P, PACK], BF16, name="wv_first", align_bytes=64, offset=2048)
                 round_wv(0, nc.scalar.copy, wv_first[:])
-            for u in range(2):
+            for u in (h, 1 - h):
                 pair = slice(2 * u, 2 * u + 2)
-                a_bank = psum.tile([P, 2, HALF], F32, name=f"a_bank{2 * h + u}")
+                a_bank = psum.tile([P, 2, HALF], F32, name=("a_bank0", "a_bank1", "rw_bank", "a_bank3")[2 * h + u])
                 for e in range(2):
                     first_product(a_bank[:, e, :], 2 * u + e, h)
-                if h == 1 and u == 1:
+                if h == 1 and u == 0:
                     vector_weight(2)
-                nc.vector.tensor_tensor(out=margins[h][:, pair, :], in0=a_bank[:], in1=y_planes[:, pair, half], op=MULT)
-                relu(hinges[h][:, pair, :], margins[h][:, pair, :])
+                nc.vector.tensor_tensor(out=margins[h][u][:], in0=a_bank[:], in1=y_planes[:, pair, half], op=MULT)
+                relu(hinges[h][:, pair, :], margins[h][u][:])
 
         def make_g(h):
             nc.vector.tensor_tensor(
                 out=by_word(g_halves[h][:]),
                 in0=by_plane(hinges[h][:]),
-                in1=by_plane(weight[:, :, h * HALF : (h + 1) * HALF]),
+                in1=by_plane(weights[h][:]),
                 op=MULT,
             )
 
@@ -275,8 +275,16 @@ def tile_attend_gml_sqh_kernel(tc, xT, wd, wv, y, cw, rw, offs, out):
         def store(q):
             nc.sync.dma_start(out=out[q * P : (q + 1) * P, :], in_=windows[q][:])
 
-        for q in (1, 2):
-            round_wv(q, nc.scalar.copy, wv_middle[:, (q - 1) * P : q * P, :])
+        wv_staged = [wv_first]
+
+        def stage_wv(q, engine_copy):
+            wv_staged.append(late.tile([P, P, PACK], BF16, name=f"wv_staged{q}", align_bytes=64, offset=1024))
+            round_wv(q, engine_copy, wv_staged[q][:])
+
+        def gpsimd_copy(out, in_):
+            nc.gpsimd.tensor_scalar(out=out, in0=in_, scalar1=1.0, scalar2=0.0, op0=MULT, op1=ADD)
+
+        stage_wv(1, nc.scalar.copy)
         make_g(0)
         quantize_wv(0, 1, wv_first)
         quantize_g(0)
@@ -285,28 +293,31 @@ def tile_attend_gml_sqh_kernel(tc, xT, wd, wv, y, cw, rw, offs, out):
         scalar_scatter(0, 0)
         g_halves.append(keep.tile([P, HALF, PACK], BF16, name="g_half1", tag="hinge0", align_bytes=64))
         make_g(1)
-        quantize_wv(1, 3, wv_middle)
+        quantize_wv(1, 2, wv_staged[1])
         quantize_g(1)
         product(1, 0)
         product(0, 1)
         product(1, 1)
-        wv_last = late.tile([P, P, PACK], BF16, name="wv_last", align_bytes=64, offset=0)
-        round_wv(3, nc.vector.tensor_copy, wv_last[:])
+        stage_wv(2, nc.vector.tensor_copy)
         fetch(1, 0, nc.vector.tensor_copy)
-        quantize_wv(3, 4, wv_last)
-        windows.append(late.tile([P, T], F32, name="window3", align_bytes=64, offset=0))
-        nc.gpsimd.memset(windows[PACK - 1][:].bitcast(U32), 0)
+        quantize_wv(2, 3, wv_staged[2])
+        stage_wv(3, gpsimd_copy)
         scalar_scatter(1, 0)
-        for q, h in ((2, 0), (3, 0), (2, 1), (3, 1)):
-            product(q, h)
+        for h in range(2):
+            product(2, h)
         for q in range(2):
             fetch(q, 1, nc.vector.tensor_copy)
-        for q in range(2):
-            vector_scatter(q, 1)
-            store(q)
+        vector_scatter(0, 1)
+        store(0)
+        quantize_wv(3, 4, wv_staged[3])
+        windows.append(late.tile([P, T], F32, name="window3", align_bytes=64, offset=0))
+        nc.gpsimd.memset(windows[PACK - 1][:].bitcast(U32), 0)
+        for h in range(2):
+            product(3, h)
+        vector_scatter(1, 1)
+        store(1)
         for q in range(2, PACK):
             fetch(q, 0, nc.scalar.copy)
-        for q in range(2, PACK):
             scalar_scatter(q, 0)
         for q in range(2, PACK):
             fetch(q, 1, nc.vector.tensor_copy)

@@ -30,19 +30,19 @@ def tile_attend_gml_sqh_kernel(tc, xT, wd, wv, y, cw, rw, offs, out):
     with ExitStack() as ctx:
         keep = ctx.enter_context(tc.tile_pool(name="keep", bufs=1))
         psum = ctx.enter_context(tc.psum_pool(name="psum", bufs=1))
-        staged = ctx.enter_context(tc.tile_pool(name="staged", bufs=1))
+        landing = ctx.enter_context(tc.tile_pool(name="landing", bufs=1))
         late = ctx.enter_context(tc.tile_pool(name="late", bufs=1))
 
         offsets = keep.tile([P, N // 16], U16, name="offsets")
         x_planes = [keep.tile([P, T], F32, name=f"x_plane{t}") for t in range(PACK)]
-        wd_raw = keep.tile([P, PACK, V], F32, name="wd_raw", tag="wd_load", align_bytes=64)
+        wd_raw = landing.tile([P, PACK, V], F32, name="wd_raw", offset=0)
         wv_raw = [
             keep.tile([P, PACK, D // 2], F32, name=f"wv_raw{u}") for u in range(2)
         ]
         y_planes = keep.tile([P, PACK, N], F32, name="y_planes")
         factor_rows = keep.tile([P, N], F32, name="factor_rows")
         rw_raw = keep.tile([P, PACK], F32, name="rw_raw")
-        windows = [keep.tile([P, T], F32, name=f"window{q}") for q in range(PACK - 1)]
+        windows = [keep.tile([P, T], F32, name=f"window{q}") for q in range(PACK)]
 
         x_rows = xT.rearrange("(p t) w -> p t w", t=PACK)
         y_rows = y.rearrange("(p t) n -> p t n", t=PACK)
@@ -64,7 +64,7 @@ def tile_attend_gml_sqh_kernel(tc, xT, wd, wv, y, cw, rw, offs, out):
         g_scales = keep.tile([P, N], U8, name="g_scales", align_bytes=64)
         identity = keep.tile([P, P], F32, name="identity")
         make_identity(nc, identity[:])
-        for q in range(PACK - 1):
+        for q in range(PACK):
             nc.vector.memset(windows[q][:].bitcast(U32), 0)
 
         neg_cw = keep.tile([P, PACK], F32, name="neg_cw")
@@ -184,10 +184,10 @@ def tile_attend_gml_sqh_kernel(tc, xT, wd, wv, y, cw, rw, offs, out):
 
         weights = [
             keep.tile([P, PACK, HALF], F32, name="weight_first", tag="wd_stage", align_bytes=64),
-            keep.tile([P, PACK, HALF], F32, name="weight_second", tag="wd_load", align_bytes=64),
+            landing.tile([P, PACK, HALF], F32, name="weight_second", offset=0),
         ]
         margins = [
-            [keep.tile([P, 2, HALF], F32, name="margin00"), late.tile([P, 2, HALF], F32, name="margin01", offset=1024)],
+            [keep.tile([P, 2, HALF], F32, name="margin00"), keep.tile([P, 2, HALF], F32, name="margin01")],
             [keep.tile([P, 2, HALF], F32, name="margin10"), keep.tile([P, 2, HALF], F32, name="margin11")],
         ]
         hinges = [keep.tile([P, PACK, HALF], F32, name=f"hinge{h}", align_bytes=64) for h in range(2)]
@@ -195,11 +195,14 @@ def tile_attend_gml_sqh_kernel(tc, xT, wd, wv, y, cw, rw, offs, out):
         wv_scales = keep.tile([P, D], U8, name="wv_scales", align_bytes=64)
         g_halves = [keep.tile([P, HALF, PACK], BF16, name="g_half0", align_bytes=64)]
 
+        cw_again = landing.tile([P, PACK], F32, name="cw_again", offset=4096)
+        nc.scalar.activation(out=cw_again[:], in_=factor_bank[:, :, P - 2], func=COPY, scale=-1.0)
+
         def vector_weight(t):
             nc.vector.scalar_tensor_tensor(
                 out=weights[1][:, t, :],
                 in0=y_planes[:, t, HALF:N],
-                scalar=neg_cw[:, t : t + 1],
+                scalar=cw_again[:, t : t + 1],
                 in1=rw_all[:, HALF:N] if t < 2 else rw_again[:].rearrange("p j n -> p (j n)"),
                 op0=MULT,
                 op1=MULT,
@@ -239,7 +242,6 @@ def tile_attend_gml_sqh_kernel(tc, xT, wd, wv, y, cw, rw, offs, out):
         bank_names = {(0, 0): "early_bank0", (1, 0): "early_bank1", (0, 1): "a_bank0", (1, 1): "a_bank1",
                       (2, 0): "a_bank2", (3, 0): "a_bank3", (2, 1): "factor_bank", (3, 1): "rw_bank"}
         banks = {}
-        shared_at = {(1, 0): 512, (2, 0): 0, (3, 0): 1024}
         dx = {}
 
         def product(q, h):
@@ -257,10 +259,7 @@ def tile_attend_gml_sqh_kernel(tc, xT, wd, wv, y, cw, rw, offs, out):
             )
 
         def fetch(q, h, engine_copy):
-            if (q, h) in shared_at:
-                dx[q, h] = staged.tile([P, HALF], F32, name=f"dx{q}{h}", offset=shared_at[q, h])
-            else:
-                dx[q, h] = keep.tile([P, HALF], F32, name=f"dx{q}{h}")
+            dx[q, h] = keep.tile([P, HALF], F32, name=f"dx{q}{h}")
             engine_copy(out=dx[q, h][:], in_=banks[q, h][:])
 
         def listed(q, h):
@@ -310,8 +309,6 @@ def tile_attend_gml_sqh_kernel(tc, xT, wd, wv, y, cw, rw, offs, out):
         vector_scatter(0, 1)
         store(0)
         quantize_wv(3, 4, wv_staged[3])
-        windows.append(late.tile([P, T], F32, name="window3", align_bytes=64, offset=0))
-        nc.gpsimd.memset(windows[PACK - 1][:].bitcast(U32), 0)
         for h in range(2):
             product(3, h)
         vector_scatter(1, 1)

@@ -31,17 +31,38 @@ def tile_attend_gml_sqh_kernel(tc, xT, wd, wv, y, cw, rw, offs, out):
         keep = ctx.enter_context(tc.tile_pool(name="keep", bufs=1))
         psum = ctx.enter_context(tc.psum_pool(name="psum", bufs=1))
         landing = ctx.enter_context(tc.tile_pool(name="landing", bufs=1))
-        late = ctx.enter_context(tc.tile_pool(name="late", bufs=1))
+        first_hinge = ctx.enter_context(tc.tile_pool(name="first_hinge", bufs=1))
+        staging = ctx.enter_context(tc.tile_pool(name="staging", bufs=1))
+
+        def entries(first, last):
+            return offsets[:, first // 16 : last // 16]
+
+        def by_plane(planes):
+            return planes.rearrange("p t (c i) -> p c t i", i=4)
+
+        def by_word(words):
+            return words.rearrange("p (c i) t -> p c t i", i=4)
+
+        def quantize(codes, scales, grouped, fmt):
+            nc.vector.quantize_mx(out=codes.bitcast(fmt), scales=scales, in_=grouped.rearrange("p n t -> p (n t)"))
+
+        def multiply(bank, w_codes, w_scales, codes, scales, fmt):
+            nc.tensor.matmul_mx(
+                out=bank,
+                lhsT=w_codes.bitcast(E4),
+                lhsT_scale=w_scales,
+                rhs=codes.bitcast(fmt),
+                rhs_scale=scales,
+                start=True,
+                stop=True,
+            )
 
         offsets = keep.tile([P, N // 16], U16, name="offsets")
         x_planes = [keep.tile([P, T], F32, name=f"x_plane{t}") for t in range(PACK)]
         wd_raw = landing.tile([P, PACK, V], F32, name="wd_raw", offset=0)
-        wv_raw = [
-            keep.tile([P, PACK, D // 2], F32, name=f"wv_raw{u}") for u in range(2)
-        ]
+        wv_raw = [keep.tile([P, PACK, D // 2], F32, name=f"wv_raw{u}") for u in range(2)]
         y_planes = keep.tile([P, PACK, N], F32, name="y_planes")
         factor_rows = keep.tile([P, N], F32, name="factor_rows")
-        rw_raw = keep.tile([P, PACK], F32, name="rw_raw")
         windows = [keep.tile([P, T], F32, name=f"window{q}") for q in range(PACK)]
 
         x_rows = xT.rearrange("(p t) w -> p t w", t=PACK)
@@ -60,210 +81,156 @@ def tile_attend_gml_sqh_kernel(tc, xT, wd, wv, y, cw, rw, offs, out):
         for u in range(2):
             nc.sync.dma_start(out=wv_raw[u][:], in_=wv_rows[:, :, u * (D // 2) : (u + 1) * (D // 2)])
 
-        g_codes = keep.tile([P, N], U32, name="g_codes", align_bytes=64)
-        g_scales = keep.tile([P, N], U8, name="g_scales", align_bytes=64)
         identity = keep.tile([P, P], F32, name="identity")
         make_identity(nc, identity[:])
         for q in range(PACK):
             nc.vector.memset(windows[q][:].bitcast(U32), 0)
 
         neg_cw = keep.tile([P, PACK], F32, name="neg_cw")
-        factor_bank = psum.tile([P, PACK, P], F32, name="factor_bank")
+        cw_bank = psum.tile([P, PACK, P], F32, name="bank_cw")
         for t in range(PACK):
-            nc.tensor.transpose(factor_bank[:, t, :], factor_rows[:, t:N:PACK], identity[:])
-        nc.scalar.activation(out=neg_cw[:], in_=factor_bank[:, :, P - 2], func=COPY, scale=-1.0)
-        rw_turn = psum.tile([P, PACK, P], F32, name="early_bank0")
+            nc.tensor.transpose(cw_bank[:, t, :], factor_rows[:, t:N:PACK], identity[:])
+        nc.scalar.activation(out=neg_cw[:], in_=cw_bank[:, :, P - 2], func=COPY, scale=-1.0)
+        rw_turn = psum.tile([P, PACK, P], F32, name="bank_e")
         for j in range(PACK):
             nc.tensor.transpose(rw_turn[:, j, :], factor_rows[:, j * P : (j + 1) * P], identity[:])
-        nc.scalar.copy(out=rw_raw[:], in_=rw_turn[:, :, P - 1])
-        rw_bank = psum.tile([P, PACK, P], F32, name="rw_bank")
-        for j in range(PACK):
-            nc.tensor.transpose(rw_bank[:, j, :], rw_raw[:, j : j + 1].to_broadcast([P, P]), identity[:])
-        rw_all = rw_bank[:].rearrange("p j n -> p (j n)")
-        rw_again = psum.tile([P, 2, P], F32, name="a_bank2")
-        for j in range(2):
-            nc.tensor.transpose(rw_again[:, j, :], rw_raw[:, 2 + j : 3 + j].to_broadcast([P, P]), identity[:])
+        rw_down = keep.tile([P, PACK], F32, name="rw_down")
+        nc.scalar.copy(out=rw_down[:], in_=rw_turn[:, :, P - 1])
+
+        def spread_rw(name, first):
+            bank = psum.tile([P, PACK - first, P], F32, name=name)
+            for j in range(first, PACK):
+                nc.tensor.transpose(bank[:, j - first, :], rw_down[:, j : j + 1].to_broadcast([P, P]), identity[:])
+            return bank[:].rearrange("p j n -> p (j n)")
+
+        rw_all = spread_rw("bank_rw", 0)
         outer = keep.tile([P, PACK, HALF], F32, name="outer")
         for t in range(PACK):
-            nc.scalar.activation(
-                out=outer[:, t, :],
-                in_=rw_all[:, 0:HALF],
-                func=COPY,
-                scale=neg_cw[:, t : t + 1],
-            )
-
-        outer_last = keep.tile([P, HALF], F32, name="outer_last")
+            nc.scalar.activation(out=outer[:, t, :], in_=rw_all[:, 0:HALF], func=COPY, scale=neg_cw[:, t : t + 1])
+        outer_last = keep.tile([P, QUARTER], F32, name="outer_last")
         nc.scalar.activation(
-            out=outer_last[:],
-            in_=rw_all[:, HALF:N],
-            func=COPY,
-            scale=neg_cw[:, PACK - 1 : PACK],
+            out=outer_last[:], in_=rw_all[:, HALF : HALF + QUARTER], func=COPY, scale=neg_cw[:, PACK - 1 : PACK]
         )
+
+        x_grouped = [keep.tile([P, HALF, PACK], BF16, name=f"x_grouped{h}", align_bytes=64) for h in range(2)]
+        x_codes = [keep.tile([P, HALF], U32, name=f"x_codes{h}", align_bytes=64) for h in range(2)]
+        x_scales = [keep.tile([P, HALF], U8, name=f"x_scales{h}", align_bytes=64) for h in range(2)]
+        for t in range(PACK):
+            nc.vector.tensor_copy(out=x_grouped[0][:, :, t], in_=x_planes[t][:].indirect(entries(0, HALF)))
+            nc.scalar.activation(out=x_grouped[1][:, :, t], in_=x_planes[t][:].indirect(entries(HALF, N)), func=COPY)
+        for h in range(2):
+            quantize(x_codes[h][:], x_scales[h][:], x_grouped[h][:], E4)
 
         wd_grouped = keep.tile([P, PACK, P, PACK], BF16, name="wd_grouped", tag="wd_stage", align_bytes=64)
         wd_to = wd_grouped[:].rearrange("p t m j -> p m j t")
         wd_from = wd_raw[:].rearrange("p j (m t) -> p m j t", t=PACK)
-        x_grouped = keep.tile([P, N, PACK], BF16, name="x_grouped", align_bytes=64)
-        x_dense = keep.tile([P, 2, QUARTER], BF16, name="x_dense")
         wd_codes = keep.tile([P, V], U32, name="wd_codes", align_bytes=64)
         wd_scales = keep.tile([P, V], U8, name="wd_scales", align_bytes=64)
-        x_codes = [keep.tile([P, HALF], U32, name=f"x_codes{h}", align_bytes=64) for h in range(2)]
-        x_scales = keep.tile([P, N], U8, name="x_scales", align_bytes=64)
-
-        def picked(t, first, last):
-            return x_planes[t][:].indirect(offsets[:, first // 16 : last // 16])
-
-        split = N - QUARTER
-        for t in range(PACK):
-            last = N if t < 2 else split
-            nc.vector.tensor_copy(out=x_grouped[:, 0:last, t], in_=picked(t, 0, last))
-            if t >= 2:
-                nc.scalar.activation(out=x_dense[:, t - 2, :], in_=picked(t, split, N), func=COPY)
-        nc.scalar.copy(out=x_grouped[:, split:N, 2:4], in_=x_dense[:].rearrange("p e n -> p n e"))
-
-        def quantize_x(h):
-            half = slice(h * HALF, (h + 1) * HALF)
-            nc.vector.quantize_mx(
-                out=x_codes[h][:].bitcast(E4),
-                scales=x_scales[:, half],
-                in_=x_grouped[:, half, :].rearrange("p n t -> p (n t)"),
-            )
-
-        quantize_x(0)
-        quantize_x(1)
         nc.vector.tensor_copy(out=wd_to[:, :, :, 0:2], in_=wd_from[:, :, :, 0:2])
         nc.vector.tensor_copy(out=wd_to[:, 0:WD_EXTRA, :, 2:4], in_=wd_from[:, 0:WD_EXTRA, :, 2:4])
         nc.scalar.copy(out=wd_to[:, WD_EXTRA:P, :, 2:4], in_=wd_from[:, WD_EXTRA:P, :, 2:4])
         for first, last in ((0, 1), (1, 2), (2, PACK)):
             cols = slice(first * P, last * P)
-            nc.vector.quantize_mx(
-                out=wd_codes[:, cols].bitcast(E4),
-                scales=wd_scales[:, cols],
-                in_=wd_grouped[:, first:last].rearrange("p t m j -> p (t m j)"),
-            )
-
-        def first_product(bank, t, h):
-            nc.tensor.matmul_mx(
-                out=bank,
-                lhsT=wd_codes[:, t * P : (t + 1) * P].bitcast(E4),
-                lhsT_scale=wd_scales[:, t * P : (t + 1) * P],
-                rhs=x_codes[h][:].bitcast(E4),
-                rhs_scale=x_scales[:, h * HALF : (h + 1) * HALF],
-                start=True,
-                stop=True,
-            )
-
-        def relu(hinge, margin):
-            nc.scalar.activation(out=hinge, in_=margin, func=RELU, bias=1.0, scale=-1.0)
-
-        def by_plane(planes):
-            return planes.rearrange("p t (c i) -> p c t i", i=4)
-
-        def by_word(words):
-            return words.rearrange("p (c i) t -> p c t i", i=4)
-
-        def quantize_wv(first, last, grouped):
-            cols = slice(first * P, last * P)
-            nc.vector.quantize_mx(
-                out=wv_codes[:, cols].bitcast(E4),
-                scales=wv_scales[:, cols],
-                in_=grouped[:].rearrange("p c j -> p (c j)"),
-            )
-
-        def quantize_g(h):
-            to = slice(h * HALF, (h + 1) * HALF)
-            nc.vector.quantize_mx(
-                out=g_codes[:, to].bitcast(E5),
-                scales=g_scales[:, to],
-                in_=g_halves[h][:].rearrange("p n t -> p (n t)"),
-            )
-
-        def round_wv(q, engine_copy, to):
-            cols = slice(q % 2 * P, (q % 2 + 1) * P)
-            engine_copy(out=by_word(to), in_=by_plane(wv_raw[q // 2][:, :, cols]))
+            quantize(wd_codes[:, cols], wd_scales[:, cols], wd_grouped[:, first:last].rearrange("p t m j -> p (t m) j"), E4)
 
         weights = [
             keep.tile([P, PACK, HALF], F32, name="weight_first", tag="wd_stage", align_bytes=64),
             landing.tile([P, PACK, HALF], F32, name="weight_second", offset=0),
         ]
-        margins = [
-            [keep.tile([P, 2, HALF], F32, name="margin00"), keep.tile([P, 2, HALF], F32, name="margin01")],
-            [keep.tile([P, 2, HALF], F32, name="margin10"), keep.tile([P, 2, HALF], F32, name="margin11")],
-        ]
-        hinges = [keep.tile([P, PACK, HALF], F32, name=f"hinge{h}", align_bytes=64) for h in range(2)]
-        wv_codes = keep.tile([P, D], U32, name="wv_codes", align_bytes=64)
-        wv_scales = keep.tile([P, D], U8, name="wv_scales", align_bytes=64)
-        g_halves = [keep.tile([P, HALF, PACK], BF16, name="g_half0", align_bytes=64)]
-
         cw_again = landing.tile([P, PACK], F32, name="cw_again", offset=4096)
-        nc.scalar.activation(out=cw_again[:], in_=factor_bank[:, :, P - 2], func=COPY, scale=-1.0)
+        nc.scalar.activation(out=cw_again[:], in_=cw_bank[:, :, P - 2], func=COPY, scale=-1.0)
 
-        def vector_weight(t):
+        def vector_weight(t, first, rw_second):
             nc.vector.scalar_tensor_tensor(
-                out=weights[1][:, t, :],
-                in0=y_planes[:, t, HALF:N],
+                out=weights[1][:, t, first:HALF],
+                in0=y_planes[:, t, HALF + first : N],
                 scalar=cw_again[:, t : t + 1],
-                in1=rw_all[:, HALF:N] if t < 2 else rw_again[:].rearrange("p j n -> p (j n)"),
+                in1=rw_second[:, first:HALF],
                 op0=MULT,
                 op1=MULT,
             )
 
         for u in range(2):
             pair = slice(2 * u, 2 * u + 2)
-            nc.gpsimd.tensor_tensor(
-                out=weights[0][:, pair, :], in0=y_planes[:, pair, 0:HALF], in1=outer[:, pair, :], op=MULT
-            )
-        nc.gpsimd.tensor_tensor(out=weights[1][:, 3, :], in0=y_planes[:, 3, HALF:N], in1=outer_last[:], op=MULT)
-        vector_weight(0)
-        vector_weight(1)
-        for h in range(2):
-            half = slice(h * HALF, (h + 1) * HALF)
-            if h == 1:
-                wv_first = late.tile([P, P, PACK], BF16, name="wv_first", align_bytes=64, offset=2048)
-                round_wv(0, nc.scalar.copy, wv_first[:])
-            for u in (h, 1 - h):
-                pair = slice(2 * u, 2 * u + 2)
-                a_bank = psum.tile([P, 2, HALF], F32, name=("a_bank0", "a_bank1", "rw_bank", "a_bank3")[2 * h + u])
-                for e in range(2):
-                    first_product(a_bank[:, e, :], 2 * u + e, h)
-                if h == 1 and u == 0:
-                    vector_weight(2)
-                nc.vector.tensor_tensor(out=margins[h][u][:], in0=a_bank[:], in1=y_planes[:, pair, half], op=MULT)
-                relu(hinges[h][:, pair, :], margins[h][u][:])
+            nc.gpsimd.tensor_tensor(out=weights[0][:, pair, :], in0=y_planes[:, pair, 0:HALF], in1=outer[:, pair, :], op=MULT)
+        nc.gpsimd.tensor_tensor(
+            out=weights[1][:, 3, 0:QUARTER], in0=y_planes[:, 3, HALF : HALF + QUARTER], in1=outer_last[:], op=MULT
+        )
+        for t in range(2):
+            vector_weight(t, 0, rw_all[:, HALF:N])
 
-        def make_g(h):
+        hinges = [
+            first_hinge.tile([P, PACK, HALF], F32, name="hinge0", align_bytes=64, offset=0),
+            keep.tile([P, PACK, HALF], F32, name="hinge1", align_bytes=64),
+        ]
+        wv_codes = keep.tile([P, D], U32, name="wv_codes", align_bytes=64)
+        wv_scales = keep.tile([P, D], U8, name="wv_scales", align_bytes=64)
+        wv_staged = {}
+
+        def round_wv(q, engine_copy, pool, offset):
+            wv_staged[q] = pool.tile([P, P, PACK], BF16, name=f"wv_staged{q}", align_bytes=64, offset=offset)
+            cols = slice(q % 2 * P, (q % 2 + 1) * P)
+            engine_copy(out=by_word(wv_staged[q][:]), in_=by_plane(wv_raw[q // 2][:, :, cols]))
+
+        def quantize_wv(q):
+            cols = slice(q * P, (q + 1) * P)
+            quantize(wv_codes[:, cols], wv_scales[:, cols], wv_staged[q][:], E4)
+
+        def hinge_of(h, u, bank_name):
+            pair = slice(2 * u, 2 * u + 2)
+            bank = psum.tile([P, 2, HALF], F32, name=bank_name)
+            for e in range(2):
+                cols = slice((2 * u + e) * P, (2 * u + e + 1) * P)
+                multiply(bank[:, e, :], wd_codes[:, cols], wd_scales[:, cols], x_codes[h][:], x_scales[h][:], E4)
+            margin = keep.tile([P, 2, HALF], F32, name=f"margin{h}{u}")
+            nc.vector.tensor_tensor(out=margin[:], in0=bank[:], in1=y_planes[:, pair, h * HALF : (h + 1) * HALF], op=MULT)
+            nc.scalar.activation(out=hinges[h][:, pair, :], in_=margin[:], func=RELU, bias=1.0, scale=-1.0)
+
+        hinge_of(0, 0, "bank_a")
+        hinge_of(0, 1, "bank_b")
+        round_wv(0, nc.scalar.copy, staging, 0)
+        hinge_of(1, 1, "bank_c")
+        hinge_of(1, 0, "bank_rw")
+        round_wv(1, nc.scalar.copy, staging, 1024)
+        rw_again = spread_rw("bank_rw", 2)
+
+        g_codes = [keep.tile([P, HALF], U32, name=f"g_codes{h}", align_bytes=64) for h in range(2)]
+        g_scales = [keep.tile([P, HALF], U8, name=f"g_scales{h}", align_bytes=64) for h in range(2)]
+        g_grouped = {}
+
+        def make_g(h, a):
+            cols = slice(a * QUARTER, (a + 1) * QUARTER)
+            if h == 0:
+                tile = keep.tile([P, QUARTER, PACK], BF16, name=f"g_first{a}", align_bytes=64)
+            else:
+                tile = first_hinge.tile([P, QUARTER, PACK], BF16, name=f"g_second{a}", align_bytes=64, offset=1024 * a)
+            g_grouped[h, a] = tile
             nc.vector.tensor_tensor(
-                out=by_word(g_halves[h][:]),
-                in0=by_plane(hinges[h][:]),
-                in1=by_plane(weights[h][:]),
-                op=MULT,
+                out=by_word(tile[:]), in0=by_plane(hinges[h][:, :, cols]), in1=by_plane(weights[h][:, :, cols]), op=MULT
             )
 
-        bank_names = {(0, 0): "early_bank0", (1, 0): "early_bank1", (0, 1): "a_bank0", (1, 1): "a_bank1",
-                      (2, 0): "a_bank2", (3, 0): "a_bank3", (2, 1): "factor_bank", (3, 1): "rw_bank"}
+        def quantize_g(h, a):
+            cols = slice(a * QUARTER, (a + 1) * QUARTER)
+            quantize(g_codes[h][:, cols], g_scales[h][:, cols], g_grouped[h, a][:], E5)
+
         banks = {}
         dx = {}
 
-        def product(q, h):
-            banks[q, h] = psum.tile([P, HALF], F32, name=bank_names[q, h])
+        def product(q, h, first, last, bank_name):
+            banks[q, h, first] = psum.tile([P, last - first], F32, name=bank_name)
             cols = slice(q * P, (q + 1) * P)
-            half = slice(h * HALF, (h + 1) * HALF)
-            nc.tensor.matmul_mx(
-                out=banks[q, h][:],
-                lhsT=wv_codes[:, cols].bitcast(E4),
-                lhsT_scale=wv_scales[:, cols],
-                rhs=g_codes[:, half].bitcast(E5),
-                rhs_scale=g_scales[:, half],
-                start=True,
-                stop=True,
+            multiply(
+                banks[q, h, first][:], wv_codes[:, cols], wv_scales[:, cols],
+                g_codes[h][:, first:last], g_scales[h][:, first:last], E5,
             )
 
-        def fetch(q, h, engine_copy):
-            dx[q, h] = keep.tile([P, HALF], F32, name=f"dx{q}{h}")
-            engine_copy(out=dx[q, h][:], in_=banks[q, h][:])
+        def fetch(q, h, first, last, engine_copy):
+            if first == 0:
+                dx[q, h] = keep.tile([P, HALF], F32, name=f"dx{q}{h}")
+            engine_copy(out=dx[q, h][:, first:last], in_=banks[q, h, first][:])
 
         def listed(q, h):
-            return windows[q][:].indirect(offsets[:, h * HALF // 16 : (h + 1) * HALF // 16])
+            return windows[q][:].indirect(entries(h * HALF, (h + 1) * HALF))
 
         def vector_scatter(q, h):
             nc.vector.tensor_copy(out=listed(q, h), in_=dx[q, h][:])
@@ -274,50 +241,51 @@ def tile_attend_gml_sqh_kernel(tc, xT, wd, wv, y, cw, rw, offs, out):
         def store(q):
             nc.sync.dma_start(out=out[q * P : (q + 1) * P, :], in_=windows[q][:])
 
-        wv_staged = [wv_first]
-
-        def stage_wv(q, engine_copy):
-            wv_staged.append(late.tile([P, P, PACK], BF16, name=f"wv_staged{q}", align_bytes=64, offset=1024))
-            round_wv(q, engine_copy, wv_staged[q][:])
-
         def gpsimd_copy(out, in_):
             nc.gpsimd.tensor_scalar(out=out, in0=in_, scalar1=1.0, scalar2=0.0, op0=MULT, op1=ADD)
 
-        stage_wv(1, nc.scalar.copy)
-        make_g(0)
-        quantize_wv(0, 1, wv_first)
-        quantize_g(0)
-        product(0, 0)
-        fetch(0, 0, nc.scalar.copy)
+        make_g(0, 0)
+        make_g(0, 1)
+        quantize_wv(0)
+        for a in range(2):
+            quantize_g(0, a)
+            product(0, 0, a * QUARTER, (a + 1) * QUARTER, ("bank_e", "bank_f")[a])
+            fetch(0, 0, a * QUARTER, (a + 1) * QUARTER, nc.scalar.copy)
         scalar_scatter(0, 0)
-        g_halves.append(keep.tile([P, HALF, PACK], BF16, name="g_half1", tag="hinge0", align_bytes=64))
-        make_g(1)
-        quantize_wv(1, 2, wv_staged[1])
-        quantize_g(1)
-        product(1, 0)
-        product(0, 1)
-        product(1, 1)
-        stage_wv(2, nc.vector.tensor_copy)
-        fetch(1, 0, nc.vector.tensor_copy)
-        quantize_wv(2, 3, wv_staged[2])
-        stage_wv(3, gpsimd_copy)
-        scalar_scatter(1, 0)
+        vector_weight(2, 0, rw_again)
+        vector_weight(3, QUARTER, rw_again)
+        make_g(1, 0)
+        make_g(1, 1)
+        quantize_wv(1)
+        product(1, 0, 0, HALF, "bank_a")
+        for a in range(2):
+            quantize_g(1, a)
+            product(0, 1, a * QUARTER, (a + 1) * QUARTER, ("bank_b", "bank_c")[a])
+        product(1, 1, 0, HALF, "bank_g")
         for h in range(2):
-            product(2, h)
-        for q in range(2):
-            fetch(q, 1, nc.vector.tensor_copy)
+            fetch(1, h, 0, HALF, nc.scalar.copy)
+        scalar_scatter(1, 0)
+        round_wv(2, nc.vector.tensor_copy, first_hinge, 0)
+        for a in range(2):
+            fetch(0, 1, a * QUARTER, (a + 1) * QUARTER, nc.vector.tensor_copy)
+        quantize_wv(2)
+        round_wv(3, gpsimd_copy, first_hinge, 0)
         vector_scatter(0, 1)
         store(0)
-        quantize_wv(3, 4, wv_staged[3])
+        product(2, 0, 0, HALF, "bank_cw")
+        product(2, 1, 0, HALF, "bank_rw")
+        whole = keep.tile([P, N], F32, name="dx_whole")
+        quantize_wv(3)
         for h in range(2):
-            product(3, h)
-        vector_scatter(1, 1)
+            nc.vector.tensor_copy(out=whole[:, h * HALF : (h + 1) * HALF], in_=banks[2, h, 0][:])
+        product(3, 0, 0, HALF, "bank_e")
+        product(3, 1, 0, HALF, "bank_f")
+        scalar_scatter(1, 1)
         store(1)
-        for q in range(2, PACK):
-            fetch(q, 0, nc.scalar.copy)
-            scalar_scatter(q, 0)
-        for q in range(2, PACK):
-            fetch(q, 1, nc.vector.tensor_copy)
-        for q in range(2, PACK):
-            vector_scatter(q, 1)
-            store(q)
+        nc.vector.tensor_copy(out=windows[2][:].indirect(offsets[:]), in_=whole[:])
+        store(2)
+        for h in range(2):
+            fetch(3, h, 0, HALF, nc.scalar.copy)
+        scalar_scatter(3, 0)
+        vector_scatter(3, 1)
+        store(3)

@@ -107,10 +107,11 @@ def tile_attend_gml_sqh_kernel(tc, xT, wd, wv, y, cw, rw, offs, out):
         outer = keep.tile([P, PACK, HALF], F32, name="outer")
         for t in range(PACK):
             nc.scalar.activation(out=outer[:, t, :], in_=rw_all[:, 0:HALF], func=COPY, scale=neg_cw[:, t : t + 1])
-        outer_last = keep.tile([P, QUARTER], F32, name="outer_last")
-        nc.scalar.activation(
-            out=outer_last[:], in_=rw_all[:, HALF : HALF + QUARTER], func=COPY, scale=neg_cw[:, PACK - 1 : PACK]
-        )
+        outer_last = keep.tile([P, 2, QUARTER], F32, name="outer_last")
+        for e in range(2):
+            nc.scalar.activation(
+                out=outer_last[:, e, :], in_=rw_all[:, HALF : HALF + QUARTER], func=COPY, scale=neg_cw[:, 2 + e : 3 + e]
+            )
 
         x_grouped = [keep.tile([P, HALF, PACK], BF16, name=f"x_grouped{h}", align_bytes=64) for h in range(2)]
         x_codes = [keep.tile([P, HALF], U32, name=f"x_codes{h}", align_bytes=64) for h in range(2)]
@@ -140,12 +141,12 @@ def tile_attend_gml_sqh_kernel(tc, xT, wd, wv, y, cw, rw, offs, out):
         cw_again = landing.tile([P, PACK], F32, name="cw_again", offset=4096)
         nc.scalar.activation(out=cw_again[:], in_=cw_bank[:, :, P - 2], func=COPY, scale=-1.0)
 
-        def vector_weight(t, first, rw_second):
+        def vector_weight(t, first, rw_part):
             nc.vector.scalar_tensor_tensor(
                 out=weights[1][:, t, first:HALF],
                 in0=y_planes[:, t, HALF + first : N],
                 scalar=cw_again[:, t : t + 1],
-                in1=rw_second[:, first:HALF],
+                in1=rw_part,
                 op0=MULT,
                 op1=MULT,
             )
@@ -154,7 +155,7 @@ def tile_attend_gml_sqh_kernel(tc, xT, wd, wv, y, cw, rw, offs, out):
             pair = slice(2 * u, 2 * u + 2)
             nc.gpsimd.tensor_tensor(out=weights[0][:, pair, :], in0=y_planes[:, pair, 0:HALF], in1=outer[:, pair, :], op=MULT)
         nc.gpsimd.tensor_tensor(
-            out=weights[1][:, 3, 0:QUARTER], in0=y_planes[:, 3, HALF : HALF + QUARTER], in1=outer_last[:], op=MULT
+            out=weights[1][:, 2:4, 0:QUARTER], in0=y_planes[:, 2:4, HALF : HALF + QUARTER], in1=outer_last[:], op=MULT
         )
         for t in range(2):
             vector_weight(t, 0, rw_all[:, HALF:N])
@@ -192,7 +193,7 @@ def tile_attend_gml_sqh_kernel(tc, xT, wd, wv, y, cw, rw, offs, out):
         hinge_of(1, 1, "bank_c")
         hinge_of(1, 0, "bank_rw")
         round_wv(1, nc.scalar.copy, staging, 1024)
-        rw_again = spread_rw("bank_rw", 2)
+        rw_last = spread_rw("bank_rw", 3)
 
         g_codes = [keep.tile([P, HALF], U32, name=f"g_codes{h}", align_bytes=64) for h in range(2)]
         g_scales = [keep.tile([P, HALF], U8, name=f"g_scales{h}", align_bytes=64) for h in range(2)]
@@ -252,8 +253,8 @@ def tile_attend_gml_sqh_kernel(tc, xT, wd, wv, y, cw, rw, offs, out):
             product(0, 0, a * QUARTER, (a + 1) * QUARTER, ("bank_e", "bank_f")[a])
             fetch(0, 0, a * QUARTER, (a + 1) * QUARTER, nc.scalar.copy)
         scalar_scatter(0, 0)
-        vector_weight(2, 0, rw_again)
-        vector_weight(3, QUARTER, rw_again)
+        for t in range(2, PACK):
+            vector_weight(t, QUARTER, rw_last)
         make_g(1, 0)
         make_g(1, 1)
         quantize_wv(1)

@@ -22,7 +22,7 @@ P = 128
 PACK = 4
 HALF = N // 2
 QUARTER = N // 4
-WD_EXTRA = 24
+WD_EXTRA = 36
 
 
 def tile_attend_gml_sqh_kernel(tc, xT, wd, wv, y, cw, rw, offs, out):
@@ -37,11 +37,11 @@ def tile_attend_gml_sqh_kernel(tc, xT, wd, wv, y, cw, rw, offs, out):
         def entries(first, last):
             return offsets[:, first // 16 : last // 16]
 
-        def by_plane(planes):
-            return planes.rearrange("p t (c i) -> p c t i", i=4)
+        def by_plane(planes, run=4):
+            return planes.rearrange("p t (c i) -> p c t i", i=run)
 
-        def by_word(words):
-            return words.rearrange("p (c i) t -> p c t i", i=4)
+        def by_word(words, run=4):
+            return words.rearrange("p (c i) t -> p c t i", i=run)
 
         def quantize(codes, scales, grouped, fmt):
             nc.vector.quantize_mx(out=codes.bitcast(fmt), scales=scales, in_=grouped.rearrange("p n t -> p (n t)"))
@@ -122,17 +122,22 @@ def tile_attend_gml_sqh_kernel(tc, xT, wd, wv, y, cw, rw, offs, out):
         for h in range(2):
             quantize(x_codes[h][:], x_scales[h][:], x_grouped[h][:], E4)
 
-        wd_grouped = keep.tile([P, PACK, P, PACK], BF16, name="wd_grouped", tag="wd_stage", align_bytes=64)
-        wd_to = wd_grouped[:].rearrange("p t m j -> p m j t")
+        wd_grouped = [
+            keep.tile([P, 2, P, PACK], BF16, name="wd_low", tag="wd_stage", align_bytes=64),
+            keep.tile([P, 2, P, PACK], BF16, name="wd_high", align_bytes=64),
+        ]
+        wd_to = [tile[:].rearrange("p t m j -> p m j t") for tile in wd_grouped]
         wd_from = wd_raw[:].rearrange("p j (m t) -> p m j t", t=PACK)
         wd_codes = keep.tile([P, V], U32, name="wd_codes", align_bytes=64)
         wd_scales = keep.tile([P, V], U8, name="wd_scales", align_bytes=64)
-        nc.vector.tensor_copy(out=wd_to[:, :, :, 0:2], in_=wd_from[:, :, :, 0:2])
-        nc.vector.tensor_copy(out=wd_to[:, 0:WD_EXTRA, :, 2:4], in_=wd_from[:, 0:WD_EXTRA, :, 2:4])
-        nc.scalar.copy(out=wd_to[:, WD_EXTRA:P, :, 2:4], in_=wd_from[:, WD_EXTRA:P, :, 2:4])
-        for first, last in ((0, 1), (1, 2), (2, PACK)):
-            cols = slice(first * P, last * P)
-            quantize(wd_codes[:, cols], wd_scales[:, cols], wd_grouped[:, first:last].rearrange("p t m j -> p (t m) j"), E4)
+        nc.vector.tensor_copy(out=wd_to[0], in_=wd_from[:, :, :, 0:2])
+        nc.vector.tensor_copy(out=wd_to[1][:, 0:WD_EXTRA], in_=wd_from[:, 0:WD_EXTRA, :, 2:4])
+        nc.scalar.copy(out=wd_to[1][:, WD_EXTRA:P], in_=wd_from[:, WD_EXTRA:P, :, 2:4])
+        for t in range(2):
+            cols = slice(t * P, (t + 1) * P)
+            quantize(wd_codes[:, cols], wd_scales[:, cols], wd_grouped[0][:, t], E4)
+        cols = slice(2 * P, PACK * P)
+        quantize(wd_codes[:, cols], wd_scales[:, cols], wd_grouped[1][:].rearrange("p t m j -> p (t m) j"), E4)
 
         weights = [
             keep.tile([P, PACK, HALF], F32, name="weight_first", tag="wd_stage", align_bytes=64),
@@ -171,7 +176,8 @@ def tile_attend_gml_sqh_kernel(tc, xT, wd, wv, y, cw, rw, offs, out):
         def round_wv(q, engine_copy, pool, offset):
             wv_staged[q] = pool.tile([P, P, PACK], BF16, name=f"wv_staged{q}", align_bytes=64, offset=offset)
             cols = slice(q % 2 * P, (q % 2 + 1) * P)
-            engine_copy(out=by_word(wv_staged[q][:]), in_=by_plane(wv_raw[q // 2][:, :, cols]))
+            run = (4, 4, 2, 1)[q]
+            engine_copy(out=by_word(wv_staged[q][:], run), in_=by_plane(wv_raw[q // 2][:, :, cols], run))
 
         def quantize_wv(q):
             cols = slice(q * P, (q + 1) * P)

@@ -23,6 +23,7 @@ PACK = 4
 HALF = N // 2
 QUARTER = N // 4
 WD_EXTRA = 36
+WEIGHT_EXTRA = 64
 
 
 def tile_attend_gml_sqh_kernel(tc, xT, wd, wv, y, cw, rw, offs, out):
@@ -106,7 +107,8 @@ def tile_attend_gml_sqh_kernel(tc, xT, wd, wv, y, cw, rw, offs, out):
         rw_all = spread_rw("bank_rw", 0)
         outer = keep.tile([P, PACK, HALF], F32, name="outer")
         for t in range(PACK):
-            nc.scalar.activation(out=outer[:, t, :], in_=rw_all[:, 0:HALF], func=COPY, scale=neg_cw[:, t : t + 1])
+            last = HALF - WEIGHT_EXTRA if t < 2 else HALF
+            nc.scalar.activation(out=outer[:, t, 0:last], in_=rw_all[:, 0:last], func=COPY, scale=neg_cw[:, t : t + 1])
         outer_last = keep.tile([P, 2, QUARTER], F32, name="outer_last")
         for e in range(2):
             nc.scalar.activation(
@@ -146,24 +148,29 @@ def tile_attend_gml_sqh_kernel(tc, xT, wd, wv, y, cw, rw, offs, out):
         cw_again = landing.tile([P, PACK], F32, name="cw_again", offset=4096)
         nc.scalar.activation(out=cw_again[:], in_=cw_bank[:, :, P - 2], func=COPY, scale=-1.0)
 
-        def vector_weight(t, first, rw_part):
+        def vector_weight(t, first, last, rw_part):
+            h = first // HALF
             nc.vector.scalar_tensor_tensor(
-                out=weights[1][:, t, first:HALF],
-                in0=y_planes[:, t, HALF + first : N],
+                out=weights[h][:, t, first - h * HALF : last - h * HALF],
+                in0=y_planes[:, t, first:last],
                 scalar=cw_again[:, t : t + 1],
                 in1=rw_part,
                 op0=MULT,
                 op1=MULT,
             )
 
-        for u in range(2):
+        for u, last in ((0, HALF - WEIGHT_EXTRA), (1, HALF)):
             pair = slice(2 * u, 2 * u + 2)
-            nc.gpsimd.tensor_tensor(out=weights[0][:, pair, :], in0=y_planes[:, pair, 0:HALF], in1=outer[:, pair, :], op=MULT)
+            nc.gpsimd.tensor_tensor(
+                out=weights[0][:, pair, 0:last], in0=y_planes[:, pair, 0:last], in1=outer[:, pair, 0:last], op=MULT
+            )
         nc.gpsimd.tensor_tensor(
             out=weights[1][:, 2:4, 0:QUARTER], in0=y_planes[:, 2:4, HALF : HALF + QUARTER], in1=outer_last[:], op=MULT
         )
         for t in range(2):
-            vector_weight(t, 0, rw_all[:, HALF:N])
+            vector_weight(t, HALF, N, rw_all[:, HALF:N])
+        for t in range(2):
+            vector_weight(t, HALF - WEIGHT_EXTRA, HALF, rw_all[:, HALF - WEIGHT_EXTRA : HALF])
 
         hinges = [
             first_hinge.tile([P, PACK, HALF], F32, name="hinge0", align_bytes=64, offset=0),
@@ -260,7 +267,7 @@ def tile_attend_gml_sqh_kernel(tc, xT, wd, wv, y, cw, rw, offs, out):
             fetch(0, 0, a * QUARTER, (a + 1) * QUARTER, nc.scalar.copy)
         scalar_scatter(0, 0)
         for t in range(2, PACK):
-            vector_weight(t, QUARTER, rw_last)
+            vector_weight(t, N - QUARTER, N, rw_last)
         make_g(1, 0)
         make_g(1, 1)
         quantize_wv(1)

@@ -59,7 +59,8 @@ def tile_attend_gml_sqh_kernel(tc, xT, wd, wv, y, cw, rw, offs, out):
             )
 
         offsets = keep.tile([P, N // 16], U16, name="offsets")
-        x_planes = [keep.tile([P, T], F32, name=f"x_plane{t}") for t in range(PACK)]
+        x_pair = keep.tile([P, 2 * T], F32, name="x_pair")
+        x_single = {t: keep.tile([P, T], F32, name=f"x_plane{t}") for t in (3, 2)}
         wd_raw = landing.tile([P, PACK, V], F32, name="wd_raw", offset=0)
         wv_raw = [keep.tile([P, PACK, D // 2], F32, name=f"wv_raw{u}") for u in range(2)]
         y_planes = keep.tile([P, PACK, N], F32, name="y_planes")
@@ -70,12 +71,12 @@ def tile_attend_gml_sqh_kernel(tc, xT, wd, wv, y, cw, rw, offs, out):
         y_rows = y.rearrange("(p t) n -> p t n", t=PACK)
         wv_rows = wv.rearrange("(p j) c -> p j c", j=PACK)
         nc.vector.memset(factor_rows[0 : P - 2, :].bitcast(U32), 0)
-        nc.sync.dma_start(out=x_planes[0][:], in_=x_rows[:, 0, :])
+        nc.sync.dma_start(out=x_pair[:], in_=x_rows[:, 0:2, :].rearrange("p t w -> p (t w)"))
         nc.sync.dma_start(offsets[:], offs)
         nc.scalar.dma_start(out=factor_rows[P - 2 : P - 1, :], in_=cw.rearrange("v o -> o v"))
         nc.scalar.dma_start(out=factor_rows[P - 1 : P, :], in_=rw[0:1, :])
-        for t in range(1, PACK):
-            nc.sync.dma_start(out=x_planes[t][:], in_=x_rows[:, t, :])
+        for t in (3, 2):
+            nc.sync.dma_start(out=x_single[t][:], in_=x_rows[:, t, :])
         nc.sync.dma_start(out=wd_raw[:], in_=wd.rearrange("(p j) c -> p j c", j=PACK))
         for u in range(2):
             nc.sync.dma_start(out=y_planes[:, 2 * u : 2 * u + 2, :], in_=y_rows[:, 2 * u : 2 * u + 2, :])
@@ -84,8 +85,9 @@ def tile_attend_gml_sqh_kernel(tc, xT, wd, wv, y, cw, rw, offs, out):
 
         identity = keep.tile([P, P], F32, name="identity")
         make_identity(nc, identity[:])
-        for q in range(PACK):
+        for q in range(PACK - 1):
             nc.vector.memset(windows[q][:].bitcast(U32), 0)
+        nc.gpsimd.memset(windows[PACK - 1][:].bitcast(U32), 0)
 
         neg_cw = keep.tile([P, PACK], F32, name="neg_cw")
         cw_bank = psum.tile([P, PACK, P], F32, name="bank_cw")
@@ -118,9 +120,14 @@ def tile_attend_gml_sqh_kernel(tc, xT, wd, wv, y, cw, rw, offs, out):
         x_grouped = [keep.tile([P, HALF, PACK], BF16, name=f"x_grouped{h}", align_bytes=64) for h in range(2)]
         x_codes = [keep.tile([P, HALF], U32, name=f"x_codes{h}", align_bytes=64) for h in range(2)]
         x_scales = [keep.tile([P, HALF], U8, name=f"x_scales{h}", align_bytes=64) for h in range(2)]
-        for t in range(PACK):
-            nc.vector.tensor_copy(out=x_grouped[0][:, :, t], in_=x_planes[t][:].indirect(entries(0, HALF)))
-            nc.scalar.activation(out=x_grouped[1][:, :, t], in_=x_planes[t][:].indirect(entries(HALF, N)), func=COPY)
+        halves = [entries(0, HALF), entries(HALF, N)]
+        nc.vector.tensor_copy(out=x_grouped[0][:, :, 0], in_=x_pair[:, 0:T].indirect(halves[0]))
+        nc.scalar.activation(out=x_grouped[1][:, :, 0], in_=x_pair[:].indirect(halves[1]), func=COPY)
+        for place, window in ((2, x_pair[:, T : 2 * T]), (3, x_single[3][:])):
+            for h in range(2):
+                nc.vector.tensor_copy(out=x_grouped[h][:, :, place], in_=window.indirect(halves[h]))
+        nc.vector.tensor_copy(out=x_grouped[0][:, :, 1], in_=x_single[2][:].indirect(halves[0]))
+        nc.scalar.activation(out=x_grouped[1][:, :, 1], in_=x_single[2][:].indirect(halves[1]), func=COPY)
         for h in range(2):
             quantize(x_codes[h][:], x_scales[h][:], x_grouped[h][:], E4)
 
@@ -128,13 +135,13 @@ def tile_attend_gml_sqh_kernel(tc, xT, wd, wv, y, cw, rw, offs, out):
             keep.tile([P, 2, P, PACK], BF16, name="wd_low", tag="wd_stage", align_bytes=64),
             keep.tile([P, 2, P, PACK], BF16, name="wd_high", align_bytes=64),
         ]
-        wd_to = [tile[:].rearrange("p t m j -> p m j t") for tile in wd_grouped]
-        wd_from = wd_raw[:].rearrange("p j (m t) -> p m j t", t=PACK)
+        wd_to = [tile[:].rearrange("p t m (b a) -> p m b a t", b=2) for tile in wd_grouped]
+        wd_from = wd_raw[:].rearrange("p (a b) (m t) -> p m b a t", b=2, t=PACK)
         wd_codes = keep.tile([P, V], U32, name="wd_codes", align_bytes=64)
         wd_scales = keep.tile([P, V], U8, name="wd_scales", align_bytes=64)
-        nc.vector.tensor_copy(out=wd_to[0], in_=wd_from[:, :, :, 0:2])
-        nc.vector.tensor_copy(out=wd_to[1][:, 0:WD_EXTRA], in_=wd_from[:, 0:WD_EXTRA, :, 2:4])
-        nc.scalar.copy(out=wd_to[1][:, WD_EXTRA:P], in_=wd_from[:, WD_EXTRA:P, :, 2:4])
+        nc.vector.tensor_copy(out=wd_to[0], in_=wd_from[:, :, :, :, 0:2])
+        nc.vector.tensor_copy(out=wd_to[1][:, 0:WD_EXTRA], in_=wd_from[:, 0:WD_EXTRA, :, :, 2:4])
+        nc.scalar.copy(out=wd_to[1][:, WD_EXTRA:P], in_=wd_from[:, WD_EXTRA:P, :, :, 2:4])
         for t in range(2):
             cols = slice(t * P, (t + 1) * P)
             quantize(wd_codes[:, cols], wd_scales[:, cols], wd_grouped[0][:, t], E4)

@@ -22,6 +22,7 @@ P = 128
 PACK = 4
 HALF = N // 2
 QUARTER = N // 4
+DMA_ALIGN = 256
 WD_EXTRA = 36
 WEIGHT_EXTRA = 64
 
@@ -59,13 +60,13 @@ def tile_attend_gml_sqh_kernel(tc, xT, wd, wv, y, cw, rw, offs, out):
             )
 
         offsets = keep.tile([P, N // 16], U16, name="offsets")
-        x_pair = keep.tile([P, 2 * T], F32, name="x_pair")
-        x_single = {t: keep.tile([P, T], F32, name=f"x_plane{t}") for t in (3, 2)}
-        wd_raw = landing.tile([P, PACK, V], F32, name="wd_raw", offset=0)
-        wv_raw = [keep.tile([P, PACK, D // 2], F32, name=f"wv_raw{u}") for u in range(2)]
-        y_planes = keep.tile([P, PACK, N], F32, name="y_planes")
+        x_pair = keep.tile([P, 2 * T], F32, name="x_pair", align_bytes=DMA_ALIGN)
+        x_single = {t: keep.tile([P, T], F32, name=f"x_plane{t}", align_bytes=DMA_ALIGN) for t in (3, 2)}
+        wd_raw = landing.tile([P, PACK, V], F32, name="wd_raw", align_bytes=DMA_ALIGN, offset=0)
+        wv_raw = [keep.tile([P, PACK, D // 2], F32, name=f"wv_raw{u}", align_bytes=DMA_ALIGN) for u in range(2)]
+        y_planes = keep.tile([P, PACK, N], F32, name="y_planes", align_bytes=DMA_ALIGN)
         factor_rows = keep.tile([P, N], F32, name="factor_rows")
-        windows = [keep.tile([P, T], F32, name=f"window{q}") for q in range(PACK)]
+        windows = [keep.tile([P, T], F32, name=f"window{q}", align_bytes=DMA_ALIGN) for q in range(PACK)]
 
         x_rows = xT.rearrange("(p t) w -> p t w", t=PACK)
         y_rows = y.rearrange("(p t) n -> p t n", t=PACK)

from contextlib import ExitStack

import concourse.mybir as mybir
from concourse.masks import make_identity

N, T, D, V = 512, 2048, 512, 512
FLOPS = 2 * D * V * N + 2 * V * D * N

F32 = mybir.dt.float32
BF16 = mybir.dt.bfloat16
U32 = mybir.dt.uint32
U16 = mybir.dt.uint16
U8 = mybir.dt.uint8
E4 = mybir.dt.float8_e4m3fn_x4
E5 = mybir.dt.float8_e5m2_x4
MULT = mybir.AluOpType.mult
ADD = mybir.AluOpType.add
COPY = mybir.ActivationFunctionType.Copy
RELU = mybir.ActivationFunctionType.Relu

P = 128
PACK = 4
HALF = N // 2
QUARTER = N // 4
DMA_ALIGN = 256
WD_EXTRA = 36
WEIGHT_EXTRA = 64


def tile_attend_gml_sqh_kernel(tc, xT, wd, wv, y, cw, rw, offs, out):
    nc = tc.nc
    with ExitStack() as ctx:
        keep = ctx.enter_context(tc.tile_pool(name="keep", bufs=1))
        psum = ctx.enter_context(tc.psum_pool(name="psum", bufs=1))
        landing = ctx.enter_context(tc.tile_pool(name="landing", bufs=1))
        first_hinge = ctx.enter_context(tc.tile_pool(name="first_hinge", bufs=1))
        staging = ctx.enter_context(tc.tile_pool(name="staging", bufs=1))

        def entries(first, last):
            return offsets[:, first // 16 : last // 16]

        def by_plane(planes, run=4):
            return planes.rearrange("p t (c i) -> p c t i", i=run)

        def by_word(words, run=4):
            return words.rearrange("p (c i) t -> p c t i", i=run)

        def quantize(codes, scales, grouped, fmt):
            nc.vector.quantize_mx(out=codes.bitcast(fmt), scales=scales, in_=grouped.rearrange("p n t -> p (n t)"))

        def multiply(bank, w_codes, w_scales, codes, scales, fmt):
            nc.tensor.matmul_mx(
                out=bank,
                lhsT=w_codes.bitcast(E4),
                lhsT_scale=w_scales,
                rhs=codes.bitcast(fmt),
                rhs_scale=scales,
                start=True,
                stop=True,
            )

        offsets = keep.tile([P, N // 16], U16, name="offsets")
        x_pair = keep.tile([P, 2 * T], F32, name="x_pair", align_bytes=DMA_ALIGN)
        x_single = {t: keep.tile([P, T], F32, name=f"x_plane{t}", align_bytes=DMA_ALIGN) for t in (3, 2)}
        wd_raw = landing.tile([P, PACK, V], F32, name="wd_raw", align_bytes=DMA_ALIGN, offset=0)
        wv_raw = [keep.tile([P, PACK, D // 2], F32, name=f"wv_raw{u}", align_bytes=DMA_ALIGN) for u in range(2)]
        y_planes = keep.tile([P, PACK, N], F32, name="y_planes", align_bytes=DMA_ALIGN)
        factor_rows = keep.tile([P, N], F32, name="factor_rows")
        windows = [keep.tile([P, T], F32, name=f"window{q}", align_bytes=DMA_ALIGN) for q in range(PACK)]

        x_rows = xT.rearrange("(p t) w -> p t w", t=PACK)
        y_rows = y.rearrange("(p t) n -> p t n", t=PACK)
        wv_rows = wv.rearrange("(p j) c -> p j c", j=PACK)
        nc.vector.memset(factor_rows[0 : P - 2, :].bitcast(U32), 0)
        nc.sync.dma_start(out=x_pair[:], in_=x_rows[:, 0:2, :].rearrange("p t w -> p (t w)"))
        nc.sync.dma_start(offsets[:], offs)
        nc.scalar.dma_start(out=factor_rows[P - 2 : P - 1, :], in_=cw.rearrange("v o -> o v"))
        nc.scalar.dma_start(out=factor_rows[P - 1 : P, :], in_=rw[0:1, :])
        for t in (3, 2):
            nc.sync.dma_start(out=x_single[t][:], in_=x_rows[:, t, :])
        nc.sync.dma_start(out=wd_raw[:], in_=wd.rearrange("(p j) c -> p j c", j=PACK))
        for u in range(2):
            nc.sync.dma_start(out=y_planes[:, 2 * u : 2 * u + 2, :], in_=y_rows[:, 2 * u : 2 * u + 2, :])
        for u in range(2):
            nc.sync.dma_start(out=wv_raw[u][:], in_=wv_rows[:, :, u * (D // 2) : (u + 1) * (D // 2)])

        identity = keep.tile([P, P], F32, name="identity")
        make_identity(nc, identity[:])
        for q in range(PACK - 1):
            nc.vector.memset(windows[q][:].bitcast(U32), 0)
        nc.gpsimd.memset(windows[PACK - 1][:].bitcast(U32), 0)

        neg_cw = keep.tile([P, PACK], F32, name="neg_cw")
        cw_bank = psum.tile([P, PACK, P], F32, name="bank_cw")
        for t in range(PACK):
            nc.tensor.transpose(cw_bank[:, t, :], factor_rows[:, t:N:PACK], identity[:])
        nc.scalar.activation(out=neg_cw[:], in_=cw_bank[:, :, P - 2], func=COPY, scale=-1.0)
        rw_turn = psum.tile([P, PACK, P], F32, name="bank_e")
        for j in range(PACK):
            nc.tensor.transpose(rw_turn[:, j, :], factor_rows[:, j * P : (j + 1) * P], identity[:])
        rw_down = keep.tile([P, PACK], F32, name="rw_down")
        nc.scalar.copy(out=rw_down[:], in_=rw_turn[:, :, P - 1])

        def spread_rw(name, first):
            bank = psum.tile([P, PACK - first, P], F32, name=name)
            for j in range(first, PACK):
                nc.tensor.transpose(bank[:, j - first, :], rw_down[:, j : j + 1].to_broadcast([P, P]), identity[:])
            return bank[:].rearrange("p j n -> p (j n)")

        rw_all = spread_rw("bank_rw", 0)
        outer = keep.tile([P, PACK, HALF], F32, name="outer")
        for t in range(PACK):
            last = HALF - WEIGHT_EXTRA if t < 2 else HALF
            nc.scalar.activation(out=outer[:, t, 0:last], in_=rw_all[:, 0:last], func=COPY, scale=neg_cw[:, t : t + 1])
        outer_last = keep.tile([P, 2, QUARTER], F32, name="outer_last")
        for e in range(2):
            nc.scalar.activation(
                out=outer_last[:, e, :], in_=rw_all[:, HALF : HALF + QUARTER], func=COPY, scale=neg_cw[:, 2 + e : 3 + e]
            )

        x_grouped = [keep.tile([P, HALF, PACK], BF16, name=f"x_grouped{h}", align_bytes=64) for h in range(2)]
        x_codes = [keep.tile([P, HALF], U32, name=f"x_codes{h}", align_bytes=64) for h in range(2)]
        x_scales = [keep.tile([P, HALF], U8, name=f"x_scales{h}", align_bytes=64) for h in range(2)]
        halves = [entries(0, HALF), entries(HALF, N)]
        nc.vector.tensor_copy(out=x_grouped[0][:, :, 0], in_=x_pair[:, 0:T].indirect(halves[0]))
        nc.scalar.activation(out=x_grouped[1][:, :, 0], in_=x_pair[:].indirect(halves[1]), func=COPY)
        for place, window in ((2, x_pair[:, T : 2 * T]), (3, x_single[3][:])):
            for h in range(2):
                nc.vector.tensor_copy(out=x_grouped[h][:, :, place], in_=window.indirect(halves[h]))
        nc.vector.tensor_copy(out=x_grouped[0][:, :, 1], in_=x_single[2][:].indirect(halves[0]))
        nc.scalar.activation(out=x_grouped[1][:, :, 1], in_=x_single[2][:].indirect(halves[1]), func=COPY)
        for h in range(2):
            quantize(x_codes[h][:], x_scales[h][:], x_grouped[h][:], E4)

        wd_grouped = [
            keep.tile([P, 2, P, PACK], BF16, name="wd_low", tag="wd_stage", align_bytes=64),
            keep.tile([P, 2, P, PACK], BF16, name="wd_high", align_bytes=64),
        ]
        wd_to = [tile[:].rearrange("p t m (b a) -> p m b a t", b=2) for tile in wd_grouped]
        wd_from = wd_raw[:].rearrange("p (a b) (m t) -> p m b a t", b=2, t=PACK)
        wd_codes = keep.tile([P, V], U32, name="wd_codes", align_bytes=64)
        wd_scales = keep.tile([P, V], U8, name="wd_scales", align_bytes=64)
        nc.vector.tensor_copy(out=wd_to[0], in_=wd_from[:, :, :, :, 0:2])
        nc.vector.tensor_copy(out=wd_to[1][:, 0:WD_EXTRA], in_=wd_from[:, 0:WD_EXTRA, :, :, 2:4])
        nc.scalar.copy(out=wd_to[1][:, WD_EXTRA:P], in_=wd_from[:, WD_EXTRA:P, :, :, 2:4])
        for t in range(2):
            cols = slice(t * P, (t + 1) * P)
            quantize(wd_codes[:, cols], wd_scales[:, cols], wd_grouped[0][:, t], E4)
        cols = slice(2 * P, PACK * P)
        quantize(wd_codes[:, cols], wd_scales[:, cols], wd_grouped[1][:].rearrange("p t m j -> p (t m) j"), E4)

        weights = [
            keep.tile([P, PACK, HALF], F32, name="weight_first", tag="wd_stage", align_bytes=64),
            landing.tile([P, PACK, HALF], F32, name="weight_second", offset=0),
        ]
        cw_again = landing.tile([P, PACK], F32, name="cw_again", offset=4096)
        nc.scalar.activation(out=cw_again[:], in_=cw_bank[:, :, P - 2], func=COPY, scale=-1.0)

        def vector_weight(t, first, last, rw_part):
            h = first // HALF
            nc.vector.scalar_tensor_tensor(
                out=weights[h][:, t, first - h * HALF : last - h * HALF],
                in0=y_planes[:, t, first:last],
                scalar=cw_again[:, t : t + 1],
                in1=rw_part,
                op0=MULT,
                op1=MULT,
            )

        for u, last in ((0, HALF - WEIGHT_EXTRA), (1, HALF)):
            pair = slice(2 * u, 2 * u + 2)
            nc.gpsimd.tensor_tensor(
                out=weights[0][:, pair, 0:last], in0=y_planes[:, pair, 0:last], in1=outer[:, pair, 0:last], op=MULT
            )
        nc.gpsimd.tensor_tensor(
            out=weights[1][:, 2:4, 0:QUARTER], in0=y_planes[:, 2:4, HALF : HALF + QUARTER], in1=outer_last[:], op=MULT
        )
        for t in range(2):
            vector_weight(t, HALF, N, rw_all[:, HALF:N])
        for t in range(2):
            vector_weight(t, HALF - WEIGHT_EXTRA, HALF, rw_all[:, HALF - WEIGHT_EXTRA : HALF])

        hinges = [
            first_hinge.tile([P, PACK, HALF], F32, name="hinge0", align_bytes=64, offset=0),
            keep.tile([P, PACK, HALF], F32, name="hinge1", align_bytes=64),
        ]
        wv_codes = keep.tile([P, D], U32, name="wv_codes", align_bytes=64)
        wv_scales = keep.tile([P, D], U8, name="wv_scales", align_bytes=64)
        wv_staged = {}

        def round_wv(q, engine_copy, pool, offset):
            wv_staged[q] = pool.tile([P, P, PACK], BF16, name=f"wv_staged{q}", align_bytes=64, offset=offset)
            cols = slice(q % 2 * P, (q % 2 + 1) * P)
            run = (4, 4, 2, 1)[q]
            engine_copy(out=by_word(wv_staged[q][:], run), in_=by_plane(wv_raw[q // 2][:, :, cols], run))

        def quantize_wv(q):
            cols = slice(q * P, (q + 1) * P)
            quantize(wv_codes[:, cols], wv_scales[:, cols], wv_staged[q][:], E4)

        def hinge_of(h, u, bank_name):
            pair = slice(2 * u, 2 * u + 2)
            bank = psum.tile([P, 2, HALF], F32, name=bank_name)
            for e in range(2):
                cols = slice((2 * u + e) * P, (2 * u + e + 1) * P)
                multiply(bank[:, e, :], wd_codes[:, cols], wd_scales[:, cols], x_codes[h][:], x_scales[h][:], E4)
            margin = keep.tile([P, 2, HALF], F32, name=f"margin{h}{u}")
            nc.vector.tensor_tensor(out=margin[:], in0=bank[:], in1=y_planes[:, pair, h * HALF : (h + 1) * HALF], op=MULT)
            nc.scalar.activation(out=hinges[h][:, pair, :], in_=margin[:], func=RELU, bias=1.0, scale=-1.0)

        hinge_of(0, 0, "bank_a")
        hinge_of(0, 1, "bank_b")
        round_wv(0, nc.scalar.copy, staging, 0)
        hinge_of(1, 1, "bank_c")
        hinge_of(1, 0, "bank_rw")
        round_wv(1, nc.scalar.copy, staging, 1024)
        rw_last = spread_rw("bank_rw", 3)

        g_codes = [keep.tile([P, HALF], U32, name=f"g_codes{h}", align_bytes=64) for h in range(2)]
        g_scales = [keep.tile([P, HALF], U8, name=f"g_scales{h}", align_bytes=64) for h in range(2)]
        g_grouped = {}

        def make_g(h, a):
            cols = slice(a * QUARTER, (a + 1) * QUARTER)
            if h == 0:
                tile = keep.tile([P, QUARTER, PACK], BF16, name=f"g_first{a}", align_bytes=64)
            else:
                tile = first_hinge.tile([P, QUARTER, PACK], BF16, name=f"g_second{a}", align_bytes=64, offset=1024 * a)
            g_grouped[h, a] = tile
            nc.vector.tensor_tensor(
                out=by_word(tile[:]), in0=by_plane(hinges[h][:, :, cols]), in1=by_plane(weights[h][:, :, cols]), op=MULT
            )

        def quantize_g(h, a):
            cols = slice(a * QUARTER, (a + 1) * QUARTER)
            quantize(g_codes[h][:, cols], g_scales[h][:, cols], g_grouped[h, a][:], E5)

        banks = {}
        dx = {}

        def product(q, h, first, last, bank_name):
            banks[q, h, first] = psum.tile([P, last - first], F32, name=bank_name)
            cols = slice(q * P, (q + 1) * P)
            multiply(
                banks[q, h, first][:], wv_codes[:, cols], wv_scales[:, cols],
                g_codes[h][:, first:last], g_scales[h][:, first:last], E5,
            )

        def fetch(q, h, first, last, engine_copy):
            if first == 0:
                dx[q, h] = keep.tile([P, HALF], F32, name=f"dx{q}{h}")
            engine_copy(out=dx[q, h][:, first:last], in_=banks[q, h, first][:])

        def listed(q, h):
            return windows[q][:].indirect(entries(h * HALF, (h + 1) * HALF))

        def vector_scatter(q, h):
            nc.vector.tensor_copy(out=listed(q, h), in_=dx[q, h][:])

        def scalar_scatter(q, h):
            nc.scalar.activation(out=listed(q, h), in_=dx[q, h][:], func=COPY)

        def store(q):
            nc.sync.dma_start(out=out[q * P : (q + 1) * P, :], in_=windows[q][:])

        def gpsimd_copy(out, in_):
            nc.gpsimd.tensor_scalar(out=out, in0=in_, scalar1=1.0, scalar2=0.0, op0=MULT, op1=ADD)

        make_g(0, 0)
        make_g(0, 1)
        quantize_wv(0)
        for a in range(2):
            quantize_g(0, a)
            product(0, 0, a * QUARTER, (a + 1) * QUARTER, ("bank_e", "bank_f")[a])
            fetch(0, 0, a * QUARTER, (a + 1) * QUARTER, nc.scalar.copy)
        scalar_scatter(0, 0)
        for t in range(2, PACK):
            vector_weight(t, N - QUARTER, N, rw_last)
        make_g(1, 0)
        make_g(1, 1)
        quantize_wv(1)
        product(1, 0, 0, HALF, "bank_a")
        for a in range(2):
            quantize_g(1, a)
            product(0, 1, a * QUARTER, (a + 1) * QUARTER, ("bank_b", "bank_c")[a])
        product(1, 1, 0, HALF, "bank_g")
        for h in range(2):
            fetch(1, h, 0, HALF, nc.scalar.copy)
        scalar_scatter(1, 0)
        round_wv(2, nc.vector.tensor_copy, first_hinge, 0)
        for a in range(2):
            fetch(0, 1, a * QUARTER, (a + 1) * QUARTER, nc.vector.tensor_copy)
        quantize_wv(2)
        round_wv(3, gpsimd_copy, first_hinge, 0)
        vector_scatter(0, 1)
        store(0)
        product(2, 0, 0, HALF, "bank_cw")
        product(2, 1, 0, HALF, "bank_rw")
        whole = keep.tile([P, N], F32, name="dx_whole")
        quantize_wv(3)
        for h in range(2):
            nc.vector.tensor_copy(out=whole[:, h * HALF : (h + 1) * HALF], in_=banks[2, h, 0][:])
        product(3, 0, 0, HALF, "bank_e")
        product(3, 1, 0, HALF, "bank_f")
        scalar_scatter(1, 1)
        store(1)
        nc.vector.tensor_copy(out=windows[2][:].indirect(offsets[:]), in_=whole[:])
        store(2)
        for h in range(2):
            fetch(3, h, 0, HALF, nc.scalar.copy)
        scalar_scatter(3, 0)
        vector_scatter(3, 1)
        store(3)
